import numpy as np
CORES = [56,61,80,85]
N = 4
T, CAPP = 1024, 512
def entries(a): return a.T.reshape(-1)
def pack(v, P): return np.ascontiguousarray(np.asarray(v, np.int32).reshape(-1, P).T)
def places(p):
    n = len(p); pl = [-1] * n; c = int(np.setdiff1d(np.arange(n), p[p != np.arange(n)])[:1].sum()); q = p.tolist()
    for k in range(n):
        if pl[c] >= 0: break
        pl[c] = k; c = q[c]
    return np.array(pl, np.int64)
def most(p):
    c = np.bincount(np.arange(N * T) // T * N + places(p) // T, minlength=N * N).reshape(N, N); return int((c - np.diag(np.diag(c))).max())
def deal(rng, m): return np.argsort(rng.random((N, m)), axis=1)
def lists(rng, how):
    n, i, G = N * T, np.arange(N), T // CAPP
    if how == "order": o = np.arange(n)
    elif how == "stride": o = np.lexsort((rng.random(n), np.arange(n) % 8))
    elif how == "mixed":
        a, t, m = rng.permutation(N), int(rng.integers(1, CAPP)), N - 1; z = a[m]; L = np.zeros((N, N), np.int64)
        for s in range(1, G + 1): L[a[:m], a[(i[:m] + s) % m]] = CAPP
        L[z, z], L[a[0], a[1]], L[a[0], z], L[z, a[1]] = T - t, CAPP - t, t, t
        lo, hi = np.zeros((N, N), np.int64), np.where(np.eye(N) > 0, T - CAPP, CAPP); lo[z, z], hi[z, z], lo[a[1], a[2]] = T - CAPP + 1, T - 1, CAPP
        for k in range(4 * N * N):
            r, u, d, v = np.append(rng.permutation(N)[:2], rng.permutation(N)[:2])
            t = int(rng.integers(0, 1 + min(hi[r, d] - L[r, d], hi[u, v] - L[u, v], L[r, v] - lo[r, v], L[u, d] - lo[u, d])))
            L[r, d] += t; L[u, v] += t; L[r, v] -= t; L[u, d] -= t
        o = np.lexsort((rng.random(n), np.concatenate([rng.permutation(np.repeat(i, l)) for l in L])))
    else:
        g, j = np.arange(G)[:, None], np.arange(CAPP)
        s = {"back": np.append(1 + np.arange(G - 1), N - 1), "full": 1 + np.arange(G), "hops": 1 + (G + np.arange(G)) % (N - 1)}[how]
        to = (i[:, None] + s) % N
        c, Q = deal(rng, T).reshape(N, G, CAPP), deal(rng, T).reshape(N, G, CAPP)
        if how == "hops": Q[:] = G * j + g
        if how == "back":
            c = np.sort(np.concatenate([np.full((N, 1), T - 1), 1 + deal(rng, T - 2), np.zeros((N, 1), np.int64)], axis=1).reshape(N, G, CAPP), axis=2); Q[:] = CAPP * g + j[::-1]
        o = np.empty(n, np.int64); o[T * to[:, :, None] + Q[to, g.T]] = T * i[:, None, None] + c
    p = np.empty(n, np.int64); p[o[:-1]] = o[1:]; p[o[-1]] = o[-1]
    return {"nx": np.stack([pack(v, 16) for v in p.reshape(N, T)])}
def setup_inputs(rng):
    return dict({"x": rng.standard_normal((N, 128, T), dtype=np.float32)}, **lists(rng, "mixed"))
def setup_inputs_back(rng):
    d = setup_inputs(rng); d.update(lists(rng, "back"))
    for k in ("x",): d[k] = (d[k].astype(np.float32) * 1048576.0).astype(d[k].dtype)
    return d
def setup_inputs_full(rng):
    d = setup_inputs(rng); d.update(lists(rng, "full"))
    for k in ("x",): d[k] = (d[k].astype(np.float32) * (1 / 1024.0)).astype(d[k].dtype)
    return d
def setup_inputs_hops(rng):
    d = setup_inputs(rng); d.update(lists(rng, "hops"))
    return d
def setup_inputs_order(rng):
    d = setup_inputs(rng); d.update(lists(rng, "order"))
    return d
def setup_inputs_stride(rng):
    d = setup_inputs(rng); d.update(lists(rng, "stride"))
    return d
def check_inputs(x):
    bad = []
    if x["nx"].min() < 0 or x["nx"].max() >= N * T: bad.append("nx out of range")
    if bad: return bad
    p = np.concatenate([entries(a) for a in x["nx"]])
    if (p == np.arange(N * T)).sum() != 1: bad.append("not exactly one column names itself")
    if not np.array_equal(np.sort(places(p)), np.arange(N * T)): bad.append("the line does not run through all columns, each once")
    elif most(p) > CAPP: bad.append("more than CAPP columns go from one rank's x to another rank's y")
    return bad
def reference(x, nx):
    X = np.concatenate(list(x), axis=1); p = np.concatenate([entries(a) for a in nx])
    pl = places(p); Y = np.zeros_like(X); Y[:, pl] = X
    return {"y": np.stack([Y[:, T * r:T * r + T] for r in range(N)])}

@@ -1,0 +1,327 @@
+from concourse.bass import DstId, RemoteDMATransfer
+from concourse.mybir import AluOpType, AxisListType, ActivationFunctionType
+
+A = AluOpType
+COPY = ActivationFunctionType.Copy
+CORES_SIM = 96
+NXE = 2
+SCRATCH = {
+    "nxs": ("dram", [128, 8], "int32"), "rnx": ("dram", [128, 8], "int32"),
+    "xall": ("sbuf", [128, 4096], "float32"), "yb": ("sbuf", [128, 1024], "float32"), "rbuf": ("sbuf", [128, 512], "float32"),
+    "xi": ("sbuf", [128, 32], "int32"),
+    "winA": ("sbuf", [128, 1024], "float32"), "winB": ("sbuf", [128, 1024], "float32"),
+    "off": ("sbuf", [128, 40], "uint16"), "off0": ("sbuf", [128, 32], "uint16"), "xo": ("sbuf", [128, 64], "uint16"),
+    "mask": ("sbuf", [128, 640], "bfloat16"), "pr": ("sbuf", [128, 640], "bfloat16"), "pb": ("sbuf", [128, 512], "bfloat16"),
+    "diag": ("sbuf", [128, 512], "bfloat16"),
+    "le": ("sbuf", [128, 2048], "bfloat16"), "gg": ("sbuf", [128, 128], "bfloat16"), "gg0": ("sbuf", [128, 128], "bfloat16"),
+    "lh": ("sbuf", [128, 128], "bfloat16"), "lt": ("sbuf", [128, 128], "bfloat16"), "ltl": ("sbuf", [128, 128], "bfloat16"),
+    "lth": ("sbuf", [128, 128], "bfloat16"), "lq": ("sbuf", [128, 128], "bfloat16"), "lq128": ("sbuf", [128, 128], "bfloat16"),
+    "rf": ("sbuf", [128, 128], "bfloat16"), "cm": ("sbuf", [128, 128], "bfloat16"), "zm": ("sbuf", [128, 128], "bfloat16"),
+    "ones": ("sbuf", [128, 128], "float32"),
+    "i_p": ("sbuf", [128, 1], "int32"), "pi": ("sbuf", [128, 16], "int32"), "pf": ("sbuf", [128, 16], "float32"),
+    "pd": ("sbuf", [128, 16], "float32"),
+    "i_row": ("sbuf", [128, 512], "float32"), "i_dg": ("sbuf", [128, 512], "float32"),
+    "i_g": ("sbuf", [128, 128], "float32"), "i_key": ("sbuf", [128, 128], "float32"), "i_low": ("sbuf", [128, 128], "float32"),
+    "i_nk": ("sbuf", [128, 128], "float32"), "i_cm": ("sbuf", [128, 128], "float32"),
+    "i_c": ("sbuf", [128, 32], "float32"), "i_id": ("sbuf", [128, 32], "float32"), "idn": ("sbuf", [128, 32], "float32"),
+    "qs": ("sbuf", [128, 16], "float32"),
+    "hi": ("sbuf", [128, 32], "int32"), "t1": ("sbuf", [128, 32], "int32"), "t2": ("sbuf", [128, 32], "int32"),
+    "lo": ("sbuf", [128, 32], "int32"), "lob": ("sbuf", [128, 32], "int32"),
+    "ha": ("sbuf", [128, 32], "float32"), "hb": ("sbuf", [128, 32], "float32"), "hc": ("sbuf", [128, 32], "float32"),
+    "hd": ("sbuf", [128, 8], "int32"), "hf": ("sbuf", [128, 8], "float32"),
+    "li": ("sbuf", [128, 128], "int32"), "lf": ("sbuf", [128, 128], "float32"),
+    "bh1": ("psum", [128, 512], "float32"), "bh2": ("psum", [128, 512], "float32"), "bt1": ("psum", [128, 512], "float32"),
+    "bt2": ("psum", [128, 512], "float32"), "be": ("psum", [128, 512], "float32"), "bhf": ("psum", [128, 512], "float32"),
+    "bz": ("psum", [128, 512], "float32"), "ba": ("psum", [128, 512], "float32"),
+}
+SEMAPHORES = ["cv", "cp", "cs", "cg", "nxl", "own", "xl0", "xl1", "nxa", "rnxa", "rq0", "rq1",
+              "rx00", "rx01", "rx10", "rx11", "fw", "nb", "loc", "st"]
+
+
+def take(mask, first, n):
+    bits = [b for b in range(16) if (mask >> b) & 1][first:first + n]
+    return sum(1 << b for b in bits)
+
+
+def plan(T, topo):
+    cores = list(T.cores)
+    out = []
+    for r, c in enumerate(cores):
+        here = [i for i, d in enumerate(cores) if topo.chip(d) == topo.chip(c)]
+        far = [i for i, d in enumerate(cores) if topo.chip(d) != topo.chip(c)]
+        k = here.index(r)
+        can = [d for d in range(CORES_SIM) if topo.chip(d) == topo.chip(c) and d not in cores
+               and all(topo.may_write(d, cores[i]) for i in far)]
+        rel = [[d for d in can if topo.die(d) == s][k] for s in (0, 1)]
+        out.append({"k": k, "nb": here[1 - k], "far": far, "rel": rel})
+    return out
+
+
+def relay_program(g, core, T, topo, r, h, k, dst):
+    S = T.sem
+    rid, pid, _ = topo.addr(dst)
+    m = topo.mask(core, dst)
+    e8 = take(m, 0, 8)
+    g.wait_ge(S.rnxa, NXE)
+    g.remote_dma(T.xi[:, 8 * r:8 * r + 8], T.rnx[:], S.nxa, S.loc, pid, rid, e8)
+    for q in (0, 1):
+        g.wait_ge(S["rq%d" % q], 8)
+        a = 1024 * r + 512 * h + 256 * q
+        g.remote_dma(T.xall[:, a:a + 256], T.rbuf[:, 256 * q:256 * q + 256], S["rx%d%d" % (k, q)], S.loc, pid, rid, e8)
+    g.wait_ge(S.loc, 24)
+
+
+def rank_program(g, core, T, topo):
+    P = plan(T, topo)
+    cores = list(T.cores)
+    rank = T.rank_of(core)
+    S = T.sem
+    if rank is None:
+        for r, p in enumerate(P):
+            for h in (0, 1):
+                if p["rel"][h] == core:
+                    relay_program(g, core, T, topo, r, h, p["k"], cores[p["far"][h]])
+        return
+    me = P[rank]
+    k, nbr = me["k"], cores[me["nb"]]
+    eng = {"v": g.vector, "p": g.tensor, "s": g.scalar, "g": g, "y": g.sync}
+    cnt = {"v": 0, "p": 0, "s": 0, "g": 0}
+    seen = {}
+
+    def wait(q, deps):
+        for d in deps:
+            if d is not None and seen.get((q, d[0]), 0) < d[1]:
+                eng[q].wait_ge(S[d[0]], d[1])
+                seen[(q, d[0])] = d[1]
+
+    def run(q, deps, name, *args, **kw):
+        wait(q, deps)
+        e = eng[q]
+        f = {"memset": lambda: e.memset, "ts": lambda: e.tensor_scalar, "tt": lambda: e.tensor_tensor, "copy": lambda: e.tensor_copy,
+             "red": lambda: e.tensor_reduce, "mm": lambda: e.matmul, "act": lambda: e.activation, "iota": lambda: e.iota}[name]()
+        f(*args, **kw).then_inc(S["c" + q], 1)
+        cnt[q] += 1
+        return ("c" + q, cnt[q])
+
+    for ch in range(8):
+        e = g.sync if ch % 2 == 0 else g.scalar
+        e.dma_start(T.nxs[16 * ch:16 * ch + 16, :], T.nx[:, 8 * ch:8 * ch + 8]).then_inc(S.nxl, 16)
+    base = 1024 * rank
+    g.sync.dma_start(T.xall[:, base:base + 512], T.x[:, 0:512]).then_inc(S.xl0, 16)
+    g.scalar.dma_start(T.xall[:, base + 512:base + 1024], T.x[:, 512:1024]).then_inc(S.xl1, 16)
+    g.sync.wait_ge(S.nxl, 128)
+    g.sync.dma_start(T.xi[:, 8 * rank:8 * rank + 8], T.nxs[:]).then_inc(S.own, 16)
+
+    def iota(buf, pattern, cm=0, flag=True):
+        if flag:
+            return run("g", [], "iota", buf[:], pattern, 0, cm, allow_small_or_imprecise_dtypes=True)
+        return run("g", [], "iota", buf[:], pattern, 0, cm)
+    ip = iota(T.i_p, [[0, 1]], 1, False)
+    ig = iota(T.i_g, [[1, 8], [0, 16]])
+    ik = iota(T.i_key, [[0, 8], [1, 2], [2, 8]])
+    ic = iota(T.i_c, [[1, 32]])
+    iid = iota(T.i_id, [[1024, 4], [16, 8]])
+    loc = 0
+    g.wait_ge(S.nxl, 128)
+    ids = [topo.addr(c) for c in me["rel"]]
+    g.remote_dma_fused([RemoteDMATransfer(dst_ids=[DstId(rid=i[0], pnc=i[1]) for i in ids], srcs=[T.nxs[:]], dsts=[T.rnx[:], T.rnx[:]],
+                                          dma_engine_mask=take(topo.mask(core, me["rel"][0]), 0, NXE), remote_sem=S.rnxa)], local_sem=S.loc)
+    loc += NXE
+    nrid, npid, _ = topo.addr(nbr)
+    nm = topo.mask(core, nbr)
+    g.remote_dma(T.xi[:, 8 * rank:8 * rank + 8], T.nxs[:], S.nxa, S.loc, npid, nrid, take(nm, 0, 8))
+    loc += 8
+    idg = iota(T.i_dg, [[0, 32], [1, 16]])
+    irow = iota(T.i_row, [[1, 512]])
+    g.wait_ge(S.xl0, 16)
+    g.wait_ge(S.xl1, 16)
+    for q in (0, 1):
+        tr = []
+        for h in (0, 1):
+            a = base + 512 * h + 256 * q
+            tr.append(RemoteDMATransfer(dst_ids=[DstId(rid=ids[h][0], pnc=ids[h][1])], srcs=[T.xall[:, a:a + 256]],
+                                        dsts=[T.rbuf[:, 256 * q:256 * q + 256]],
+                                        dma_engine_mask=take(topo.mask(core, me["rel"][h]), 8 * h, 8), remote_sem=S["rq%d" % q]))
+        g.remote_dma_fused(tr, local_sem=S.loc)
+        loc += 16
+    g.remote_dma(T.xall[:, base:base + 1024], T.xall[:, base:base + 1024], S.nb, S.loc, npid, nrid, take(nm, 0, 16))
+    loc += 16
+    ilow = iota(T.i_low, [[0, 8], [1, 16]])
+    ink = iota(T.i_nk, [[1, 2], [0, 8], [2, 8]])
+    icm = iota(T.i_cm, [[0, 2], [1, 8], [0, 8]])
+    for q in (0, 1):
+        for s, fr in enumerate(me["far"]):
+            g.wait_ge(S["rx%d%d" % (s, q)], 8)
+            a = 1024 * fr + 512 * k + 256 * q
+            g.remote_dma(T.xall[:, a:a + 256], T.xall[:, a:a + 256], S.fw, S.loc, npid, nrid, take(nm, 0, 16))
+            loc += 16
+    g.wait_ge(S.loc, loc)
+
+    V, PE, SC = "v", "p", "s"
+    run(V, [], "memset", T.ones[:], 1.0)
+    t = run(V, [], "memset", T.le[:], 0.0)
+    le0 = t
+    for c, (sh, an) in enumerate([(4, 7), (3, 1), (0, 7), (0, 15), (3, 15)] + [(i, 1) for i in range(7)]):
+        t = run(V, [ip], "ts", T.pi[:, c:c + 1], T.i_p[:], sh, an, A.arith_shift_right, A.bitwise_and)
+    t = run(V, [t], "copy", T.pf[:, 0:12], T.pi[:, 0:12])
+    t = run(V, [t], "ts", T.pd[:, 0:7], T.pf[:, 5:12], -512.0, 768.0, A.mult, A.add)
+    run(V, [t], "ts", T.pd[:, 8:9], T.pf[:, 0:1], 2.0, None, A.mult)
+    run(V, [t], "ts", T.pd[:, 9:10], T.pf[:, 0:1], 2.0, 1.0, A.mult, A.add)
+    run(V, [t], "ts", T.pd[:, 10:11], T.pf[:, 0:1], 128.0, T.pf[:, 3:4], A.mult, A.add)
+    t = run(V, [t], "ts", T.pd[:, 11:12], T.pf[:, 1:2], -1.0, 1.0, A.mult, A.add)
+    t = run(V, [t], "ts", T.pd[:, 12:13], T.pd[:, 11:12], -256.0, None, A.mult)
+    gd = t
+    pg, pfl, ps, pq, pk = [T.pf[:, c:c + 1] for c in range(5)]
+    gg0 = run(V, [gd, ig], "ts", T.gg0[:], T.i_g[:], pg, T.pd[:, 11:12], A.is_equal, A.mult)
+    for q in range(16):
+        les = run(SC, [gg0, le0], "act", T.le[:, 128 * q + q:128 * q + 128:16], T.gg0[:, q:128:16], COPY)
+    run(V, [], "ts", T.gg[:], T.i_g[:], pg, None, A.is_equal)
+    run(V, [], "ts", T.lh[:], T.i_g[:], pg, pfl, A.is_equal, A.mult)
+    run(V, [ik], "ts", T.lt[:], T.i_key[:], pk, None, A.is_equal)
+    run(V, [], "ts", T.ltl[:], T.i_key[:], T.pd[:, 8:9], None, A.is_equal)
+    run(V, [], "ts", T.lth[:], T.i_key[:], T.pd[:, 9:10], None, A.is_equal)
+    run(V, [ic], "copy", T.off0[:], T.i_c[:])
+    run(V, [], "ts", T.qs[:], T.i_c[:, 0:16], 0.0, ps, A.mult, A.add)
+    run(V, [iid], "ts", T.idn[:], T.i_id[:], T.pd[:, 10:11], None, A.add)
+    t = run(V, [idg], "ts", T.diag[:], T.i_dg[:], pq, None, A.is_equal)
+    t = run(V, [], "ts", T.pd[:, 13:14], ps, pfl, T.pd[:, 12:13], A.mult, A.add)
+    t = run(V, [t, irow], "ts", T.winA[:, 512:1024], T.i_row[:], T.pd[:, 11:12], T.pd[:, 13:14], A.mult, A.add)
+    idb = run(SC, [t], "act", T.winB[:, 512:1024], T.winA[:, 512:1024], COPY)
+
+    def ca():
+        run(V, [ilow], "ts", T.lq[:], T.i_low[:], pq, None, A.is_equal)
+
+    def cb():
+        run(V, [], "ts", T.lq128[:], T.i_low[:], pq, 128.0, A.is_equal, A.mult)
+
+    def cc():
+        run(V, [ink], "ts", T.rf[:], T.i_nk[:], pk, None, A.is_equal)
+
+    def cd():
+        run(V, [icm], "ts", T.cm[:], T.i_cm[:], pg, None, A.is_equal)
+    hooks = {2: ca, 3: cb, 4: cc, 5: cd}
+
+    wait(V, [("nxa", 24), ("own", 16), t])
+    X = T.xi[:]
+    h0 = run(V, [], "ts", T.hi[:], X, 7, 7, A.arith_shift_right, A.bitwise_and)
+    run(V, [], "ts", T.t1[:], X, 3, 0x180, A.arith_shift_right, A.bitwise_and)
+    t2 = run(V, [], "ts", T.t2[:], X, 0x7F, None, A.bitwise_and)
+    ghi = run(V, [h0], "tt", T.pr[:, 0:512], T.hi[:].indirect(T.off0[:]), T.diag[:], A.mult)
+    lo = run(V, [t2], "tt", T.lo[:], T.t1[:], T.t2[:], A.add)
+    eq = run(V, [], "tt", T.ha[:], X, T.idn[:], A.is_equal)
+    lob = run(V, [lo], "ts", T.lob[:], T.lo[:], 256.0, None, A.subtract)
+    hb = run(V, [eq], "tt", T.hb[:], T.ha[:], T.idn[:], A.mult)
+    glo = run(V, [lob], "tt", T.pb[:], T.lob[:].indirect(T.off0[:]), T.diag[:], A.mult)
+    hc = run(V, [hb], "tt", T.hc[:], T.hb[:], X, A.subtract)
+    offS = run(V, [], "copy", T.off[:, 0:32], T.lo[:])
+    hs = run(V, [hc], "red", T.hf[:, 2:3], T.hc[:], AxisListType.X, A.add)
+    ph1 = run(PE, [ghi], "mm", T.bh1[:, 0:256], T.gg[:], T.pr[:, 0:256], True, True)
+    ph2 = run(PE, [], "mm", T.bh2[:, 0:256], T.gg[:], T.pr[:, 256:512], True, True)
+    run(PE, [], "mm", T.bt1[:, 0:256], T.lth[:], T.pr[:, 0:256], True, False)
+    run(PE, [], "mm", T.bt2[:, 0:256], T.lth[:], T.pr[:, 256:512], True, False)
+    pt1 = run(PE, [glo], "mm", T.bt1[:, 0:256], T.ltl[:], T.pb[:, 0:256], False, True)
+    pt2 = run(PE, [], "mm", T.bt2[:, 0:256], T.ltl[:], T.pb[:, 256:512], False, True)
+    php = run(PE, [hs], "mm", T.bz[:, 0:1], T.ones[:], T.hf[:, 2:3], True, True)
+    run(SC, [pt1], "act", T.winA[:, 0:256], T.bt1[:, 0:256], COPY)
+    tab = run(SC, [pt2], "act", T.winA[:, 256:512], T.bt2[:, 0:256], COPY)
+    m1 = run(V, [ph1], "ts", T.mask[:, 0:256], T.bh1[:, 0:256], ps, None, A.is_equal)
+    m2 = run(V, [ph2], "ts", T.mask[:, 256:512], T.bh2[:, 0:256], ps, None, A.is_equal)
+    hd = run(V, [php], "ts", T.hd[:, 0:1], T.bz[:, 0:1], float(4096 * 4095 // 2), None, A.add)
+
+    def pend0():
+        a = run(V, [hd], "ts", T.hd[:, 1:2], T.hd[:, 0:1], 7, 7, A.arith_shift_right, A.bitwise_and)
+        run(V, [], "ts", T.hd[:, 2:3], T.hd[:, 0:1], 3, 0x180, A.arith_shift_right, A.bitwise_and)
+        b = run(V, [], "ts", T.hd[:, 3:4], T.hd[:, 0:1], 0x7F, None, A.bitwise_and)
+        c = run(V, [a], "copy", T.hf[:, 1:2], T.hd[:, 1:2])
+        d = run(V, [b], "tt", T.hf[:, 0:1], T.hd[:, 2:3], T.hd[:, 3:4], A.add)
+        run(V, [c], "ts", T.mask[:, 512:528], T.qs[:], T.hf[:, 1:2], None, A.is_equal)
+        return run(V, [d], "ts", T.off[:, 32:33], T.hf[:, 0:1], T.pd[:, 0:1], 256.0, A.add, A.subtract)
+    pending = pend0
+    win = [T.winA, T.winB]
+    LE = [T.le[:, 128 * q:128 * q + 128] for q in range(16)]
+
+    def gather(w, a, b, deps):
+        return run(V, deps, "tt", T.pr[:, 16 * a:16 * b], w.indirect(T.off[:, a:b]), T.mask[:, 16 * a:16 * b], A.mult)
+
+    def extract(a, b, deps):
+        for q in range(16):
+            e = run(PE, deps, "mm", T.be[:, 0:b - a], LE[q], T.pr[:, 16 * a + q:16 * b:16], q == 0, q == 15)
+        return e
+
+    wait(PE, [les])
+    wait(V, [idb])
+    for i in range(10):
+        nF = 1 if i <= 7 else 1 << (i - 7)
+        w, nw = win[i % 2][:], win[(i + 1) % 2]
+        lastr, table = i == 9, not (i == 9 and rank == 0)
+        if table:
+            g1 = gather(w, 0, 16, [tab, offS, m1])
+            pt1 = run(PE, [g1], "mm", T.bt1[:, 0:256], T.lt[:], T.pr[:, 0:256], True, True)
+            run(SC, [pt1], "act", nw[:, 0:256], T.bt1[:, 0:256], COPY)
+            if not lastr:
+                ph1 = run(PE, [], "mm", T.bh1[:, 0:256], T.lh[:], T.pr[:, 0:256], True, True)
+            pF = pending()
+            g2 = gather(w, 16, 32 + nF, [m2, pF])
+            pt2 = run(PE, [g2], "mm", T.bt2[:, 0:256], T.lt[:], T.pr[:, 256:512], True, True)
+            tab = run(SC, [pt2], "act", nw[:, 256:512], T.bt2[:, 0:256], COPY)
+        else:
+            pF = pending()
+            g2 = gather(w, 32, 32 + nF, [tab, pF])
+        new = 32 if i <= 6 else 32 + nF
+        if not lastr:
+            ph2 = run(PE, [], "mm", T.bh2[:, 0:256], T.lh[:], T.pr[:, 256:512], True, True)
+            pe = extract(0, 32 + nF, [])
+            e0 = 32
+        else:
+            pe = extract(32, 32 + nF, [g2])
+            e0 = 0
+        phf = run(PE, [], "mm", T.bhf[:, 0:16 * nF], T.lh[:], T.pr[:, 512:512 + 16 * nF], True, True)
+        if not lastr:
+            m1 = run(V, [ph1, g1], "ts", T.mask[:, 0:256], T.bh1[:, 0:256], ps, None, A.is_equal)
+            m2 = run(V, [ph2, g2], "ts", T.mask[:, 256:512], T.bh2[:, 0:256], ps, None, A.is_equal)
+        if i in hooks:
+            hooks[i]()
+        if not lastr:
+            offS = run(V, [pe], "ts", T.off[:, 0:32], T.be[:, 0:32], 256.0, None, A.add)
+
+        def pend(pe=pe, phf=phf, i=i, nF=nF, new=new, e0=e0):
+            sc = T.pd[:, i + 1:i + 2] if i + 1 <= 6 else 256.0
+            run(V, [pe], "ts", T.off[:, new:new + nF], T.be[:, e0:e0 + nF], sc, None, A.add)
+            return run(V, [phf], "ts", T.mask[:, 16 * new:16 * (new + nF)], T.bhf[:, 0:16 * nF], ps, None, A.is_equal)
+        pending = pend
+    w = win[0][:] if rank else win[1][:, 512:1024]
+    steps = max(1, rank)
+    for s in range(steps):
+        pF = pending()
+        gF = gather(w, 32, 40, [tab, pF])
+        if s < steps - 1:
+            pe = extract(32, 40, [gF])
+            phf = run(PE, [], "mm", T.bhf[:, 0:128], T.lh[:], T.pr[:, 512:640], True, True)
+
+            def pend(pe=pe, phf=phf):
+                run(V, [pe], "ts", T.off[:, 32:40], T.be[:, 0:8], 256.0, None, A.add)
+                return run(V, [phf], "ts", T.mask[:, 512:640], T.bhf[:, 0:128], ps, None, A.is_equal)
+            pending = pend
+    z = run(PE, [gF], "mm", T.bz[:, 0:128], T.pr[:, 512:640], T.rf[:], True, True)
+    zm = run(V, [z], "tt", T.zm[:], T.bz[:, 0:128], T.cm[:], A.mult)
+    pl = run(PE, [zm], "mm", T.ba[:, 0:64], T.lq[:], T.zm[:, 0:64], True, True)
+    run(PE, [], "mm", T.bz[:, 128:192], T.lq[:], T.zm[:, 0:64], True, False)
+    pb = run(PE, [], "mm", T.bz[:, 128:192], T.lq128[:], T.zm[:, 64:128], False, True)
+    t = run(V, [pl], "ts", T.li[:, 0:64], T.ba[:, 0:64], 256.0, None, A.add)
+    t = run(V, [t], "ts", T.li[:, 64:128], T.li[:, 0:64], 0x180, None, A.bitwise_and)
+    t = run(V, [t], "ts", T.lf[:, 0:64], T.li[:, 64:128], 7.0, 256.0, A.mult, A.add)
+    t = run(V, [t, pb], "tt", T.lf[:, 64:128], T.lf[:, 0:64], T.bz[:, 128:192], A.add)
+    xo = run(V, [t], "copy", T.xo[:], T.lf[:, 64:128])
+    xs = [("xl0", 16), ("xl1", 16), ("nb", 16), ("rx00", 8), ("rx01", 8), ("rx10", 8), ("rx11", 8), ("fw", 64)]
+    wait(SC, xs)
+    wait(V, xs)
+    got = []
+    for q in (0, 1):
+        a, b = 256 * q, 512 + 256 * q
+        got.append((a, run(V, [xo], "copy", T.yb[:, a:a + 256], T.xall[:].indirect(T.xo[:, a // 16:a // 16 + 16]))))
+        got.append((b, run(SC, [xo], "act", T.yb[:, b:b + 256], T.xall[:].indirect(T.xo[:, b // 16:b // 16 + 16]), COPY)))
+    for a, tok in got:
+        wait("y", [tok])
+        g.sync.dma_start(T.y[:, a:a + 256], T.yb[:, a:a + 256]).then_inc(S.st, 16)
+    g.sync.wait_ge(S.st, 64)
+    wait("v", [("cv", cnt["v"]), ("cp", cnt["p"]), ("cs", cnt["s"]), ("cg", cnt["g"])])

@@ -5,6 +5,7 @@ A = AluOpType
 COPY = ActivationFunctionType.Copy
 CORES_SIM = 96
 NXE = 2
+W896 = [(0.00111389160156, 0.0000021755695343), (0.142578125, 0.00027942657470703125)]
 SCRATCH = {
     "nxs": ("dram", [128, 8], "int32"), "rnx": ("dram", [128, 8], "int32"),
     "xall": ("sbuf", [128, 4096], "float32"), "yb": ("sbuf", [128, 1024], "float32"), "rbuf": ("sbuf", [128, 512], "float32"),
@@ -15,21 +16,18 @@ SCRATCH = {
     "diag": ("sbuf", [128, 512], "bfloat16"),
     "le": ("sbuf", [128, 2048], "bfloat16"), "gg": ("sbuf", [128, 128], "bfloat16"), "gg0": ("sbuf", [128, 128], "bfloat16"),
     "lh": ("sbuf", [128, 128], "bfloat16"), "lt": ("sbuf", [128, 128], "bfloat16"), "ltl": ("sbuf", [128, 128], "bfloat16"),
-    "lth": ("sbuf", [128, 128], "bfloat16"), "lq": ("sbuf", [128, 128], "bfloat16"), "lq128": ("sbuf", [128, 128], "bfloat16"),
+    "lth": ("sbuf", [128, 128], "bfloat16"), "lq": ("sbuf", [128, 128], "bfloat16"), "lqs": ("sbuf", [128, 512], "bfloat16"),
     "rf": ("sbuf", [128, 128], "bfloat16"), "cm": ("sbuf", [128, 128], "bfloat16"), "zm": ("sbuf", [128, 128], "bfloat16"),
     "ones": ("sbuf", [128, 128], "float32"),
     "i_p": ("sbuf", [128, 1], "int32"), "pi": ("sbuf", [128, 16], "int32"), "pf": ("sbuf", [128, 16], "float32"),
-    "pd": ("sbuf", [128, 16], "float32"),
-    "i_row": ("sbuf", [128, 512], "float32"), "i_dg": ("sbuf", [128, 512], "float32"),
+    "pd": ("sbuf", [128, 24], "float32"), "i_m": ("sbuf", [128, 128], "float32"),
     "i_g": ("sbuf", [128, 128], "float32"), "i_key": ("sbuf", [128, 128], "float32"), "i_low": ("sbuf", [128, 128], "float32"),
     "i_nk": ("sbuf", [128, 128], "float32"), "i_cm": ("sbuf", [128, 128], "float32"),
     "i_c": ("sbuf", [128, 32], "float32"), "i_id": ("sbuf", [128, 32], "float32"), "idn": ("sbuf", [128, 32], "float32"),
     "qs": ("sbuf", [128, 16], "float32"),
-    "hi": ("sbuf", [128, 32], "int32"), "t1": ("sbuf", [128, 32], "int32"), "t2": ("sbuf", [128, 32], "int32"),
-    "lo": ("sbuf", [128, 32], "int32"), "lob": ("sbuf", [128, 32], "int32"),
-    "ha": ("sbuf", [128, 32], "float32"), "hb": ("sbuf", [128, 32], "float32"), "hc": ("sbuf", [128, 32], "float32"),
+    "xw": ("sbuf", [128, 160], "int32"), "hw": ("sbuf", [128, 96], "float32"),
     "hd": ("sbuf", [128, 8], "int32"), "hf": ("sbuf", [128, 8], "float32"),
-    "li": ("sbuf", [128, 128], "int32"), "lf": ("sbuf", [128, 128], "float32"),
+    "li": ("sbuf", [128, 64], "int32"), "lf": ("sbuf", [128, 64], "float32"),
     "bh1": ("psum", [128, 512], "float32"), "bh2": ("psum", [128, 512], "float32"), "bt1": ("psum", [128, 512], "float32"),
     "bt2": ("psum", [128, 512], "float32"), "be": ("psum", [128, 512], "float32"), "bhf": ("psum", [128, 512], "float32"),
     "bz": ("psum", [128, 512], "float32"), "ba": ("psum", [128, 512], "float32"),
@@ -131,8 +129,10 @@ def rank_program(g, core, T, topo):
     nm = topo.mask(core, nbr)
     g.remote_dma(T.xi[:, 8 * rank:8 * rank + 8], T.nxs[:], S.nxa, S.loc, npid, nrid, take(nm, 0, 8))
     loc += 8
-    idg = iota(T.i_dg, [[0, 32], [1, 16]])
-    irow = iota(T.i_row, [[1, 512]])
+    ilow = iota(T.i_low, [[0, 8], [1, 16]])
+    im = iota(T.i_m, [[1, 128]])
+    ink = iota(T.i_nk, [[1, 2], [0, 8], [2, 8]])
+    icm = iota(T.i_cm, [[0, 2], [1, 8], [0, 8]])
     g.wait_ge(S.xl0, 16)
     g.wait_ge(S.xl1, 16)
     for q in (0, 1):
@@ -146,9 +146,6 @@ def rank_program(g, core, T, topo):
         loc += 16
     g.remote_dma(T.xall[:, base:base + 1024], T.xall[:, base:base + 1024], S.nb, S.loc, npid, nrid, take(nm, 0, 16))
     loc += 16
-    ilow = iota(T.i_low, [[0, 8], [1, 16]])
-    ink = iota(T.i_nk, [[1, 2], [0, 8], [2, 8]])
-    icm = iota(T.i_cm, [[0, 2], [1, 8], [0, 8]])
     for q in (0, 1):
         for s, fr in enumerate(me["far"]):
             g.wait_ge(S["rx%d%d" % (s, q)], 8)
@@ -159,159 +156,184 @@ def rank_program(g, core, T, topo):
 
     V, PE, SC = "v", "p", "s"
     run(V, [], "memset", T.ones[:], 1.0)
-    t = run(V, [], "memset", T.le[:], 0.0)
-    le0 = t
+    le0 = run(V, [], "memset", T.le[:], 0.0)
     for c, (sh, an) in enumerate([(4, 7), (3, 1), (0, 7), (0, 15), (3, 15)] + [(i, 1) for i in range(7)]):
         t = run(V, [ip], "ts", T.pi[:, c:c + 1], T.i_p[:], sh, an, A.arith_shift_right, A.bitwise_and)
     t = run(V, [t], "copy", T.pf[:, 0:12], T.pi[:, 0:12])
-    t = run(V, [t], "ts", T.pd[:, 0:7], T.pf[:, 5:12], -512.0, 768.0, A.mult, A.add)
-    run(V, [t], "ts", T.pd[:, 8:9], T.pf[:, 0:1], 2.0, None, A.mult)
-    run(V, [t], "ts", T.pd[:, 9:10], T.pf[:, 0:1], 2.0, 1.0, A.mult, A.add)
-    run(V, [t], "ts", T.pd[:, 10:11], T.pf[:, 0:1], 128.0, T.pf[:, 3:4], A.mult, A.add)
-    t = run(V, [t], "ts", T.pd[:, 11:12], T.pf[:, 1:2], -1.0, 1.0, A.mult, A.add)
-    t = run(V, [t], "ts", T.pd[:, 12:13], T.pd[:, 11:12], -256.0, None, A.mult)
-    gd = t
     pg, pfl, ps, pq, pk = [T.pf[:, c:c + 1] for c in range(5)]
-    gg0 = run(V, [gd, ig], "ts", T.gg0[:], T.i_g[:], pg, T.pd[:, 11:12], A.is_equal, A.mult)
+
+    def col(c):
+        return T.pd[:, c:c + 1]
+    t = run(V, [t], "ts", col(11), pfl, -1.0, 1.0, A.mult, A.add)
+    run(V, [t], "ts", T.pd[:, 0:7], T.pf[:, 5:12], -512.0, 768.0, A.mult, A.add)
+    gg0 = run(V, [t, ig], "ts", T.gg0[:], T.i_g[:], pg, col(11), A.is_equal, A.mult)
     for q in range(16):
         les = run(SC, [gg0, le0], "act", T.le[:, 128 * q + q:128 * q + 128:16], T.gg0[:, q:128:16], COPY)
+    run(V, [], "ts", col(8), pg, 2.0, None, A.mult)
+    run(V, [], "ts", col(9), pg, 2.0, 1.0, A.mult, A.add)
+    run(V, [], "ts", col(10), pg, 128.0, pq, A.mult, A.add)
+    t = run(V, [], "ts", col(16), ps, pfl, None, A.mult)
     run(V, [], "ts", T.gg[:], T.i_g[:], pg, None, A.is_equal)
     run(V, [], "ts", T.lh[:], T.i_g[:], pg, pfl, A.is_equal, A.mult)
+    for b in range(4):
+        u = run(V, [t], "ts", col(12 + b), col(11), 128.0 * b - 256.0, col(16), A.mult, A.add)
     run(V, [ik], "ts", T.lt[:], T.i_key[:], pk, None, A.is_equal)
-    run(V, [], "ts", T.ltl[:], T.i_key[:], T.pd[:, 8:9], None, A.is_equal)
-    run(V, [], "ts", T.lth[:], T.i_key[:], T.pd[:, 9:10], None, A.is_equal)
+    run(V, [], "ts", T.ltl[:], T.i_key[:], col(8), None, A.is_equal)
+    run(V, [], "ts", T.lth[:], T.i_key[:], col(9), None, A.is_equal)
     run(V, [ic], "copy", T.off0[:], T.i_c[:])
     run(V, [], "ts", T.qs[:], T.i_c[:, 0:16], 0.0, ps, A.mult, A.add)
-    run(V, [iid], "ts", T.idn[:], T.i_id[:], T.pd[:, 10:11], None, A.add)
-    t = run(V, [idg], "ts", T.diag[:], T.i_dg[:], pq, None, A.is_equal)
-    t = run(V, [], "ts", T.pd[:, 13:14], ps, pfl, T.pd[:, 12:13], A.mult, A.add)
-    t = run(V, [t, irow], "ts", T.winA[:, 512:1024], T.i_row[:], T.pd[:, 11:12], T.pd[:, 13:14], A.mult, A.add)
+    run(V, [iid], "ts", T.idn[:], T.i_id[:], col(10), None, A.add)
+    for b in range(4):
+        run(V, [ilow], "ts", T.diag[:, 128 * b:128 * b + 128], T.i_low[:], pq, None, A.is_equal)
+    for b in range(4):
+        t = run(V, [u, im], "ts", T.winA[:, 512 + 128 * b:640 + 128 * b], T.i_m[:], col(11), col(12 + b), A.mult, A.add)
     idb = run(SC, [t], "act", T.winB[:, 512:1024], T.winA[:, 512:1024], COPY)
+    run(V, [], "ts", T.lq[:], T.i_low[:], pq, None, A.is_equal)
+    for f in (0, 1):
+        for j in (0, 1):
+            b = 2 * f + j
+            run(V, [], "ts", T.lqs[:, 128 * b:128 * b + 128], T.i_low[:], pq, W896[f][j], A.is_equal, A.mult)
+    run(V, [ink], "ts", T.rf[:], T.i_nk[:], pk, None, A.is_equal)
+    t = run(V, [icm], "ts", T.cm[:], T.i_cm[:], pg, None, A.is_equal)
 
-    def ca():
-        run(V, [ilow], "ts", T.lq[:], T.i_low[:], pq, None, A.is_equal)
-
-    def cb():
-        run(V, [], "ts", T.lq128[:], T.i_low[:], pq, 128.0, A.is_equal, A.mult)
-
-    def cc():
-        run(V, [ink], "ts", T.rf[:], T.i_nk[:], pk, None, A.is_equal)
-
-    def cd():
-        run(V, [icm], "ts", T.cm[:], T.i_cm[:], pg, None, A.is_equal)
-    hooks = {2: ca, 3: cb, 4: cc, 5: cd}
-
-    wait(V, [("nxa", 24), ("own", 16), t])
-    X = T.xi[:]
-    h0 = run(V, [], "ts", T.hi[:], X, 7, 7, A.arith_shift_right, A.bitwise_and)
-    run(V, [], "ts", T.t1[:], X, 3, 0x180, A.arith_shift_right, A.bitwise_and)
-    t2 = run(V, [], "ts", T.t2[:], X, 0x7F, None, A.bitwise_and)
-    ghi = run(V, [h0], "tt", T.pr[:, 0:512], T.hi[:].indirect(T.off0[:]), T.diag[:], A.mult)
-    lo = run(V, [t2], "tt", T.lo[:], T.t1[:], T.t2[:], A.add)
-    eq = run(V, [], "tt", T.ha[:], X, T.idn[:], A.is_equal)
-    lob = run(V, [lo], "ts", T.lob[:], T.lo[:], 256.0, None, A.subtract)
-    hb = run(V, [eq], "tt", T.hb[:], T.ha[:], T.idn[:], A.mult)
-    glo = run(V, [lob], "tt", T.pb[:], T.lob[:].indirect(T.off0[:]), T.diag[:], A.mult)
-    hc = run(V, [hb], "tt", T.hc[:], T.hb[:], X, A.subtract)
-    offS = run(V, [], "copy", T.off[:, 0:32], T.lo[:])
-    hs = run(V, [hc], "red", T.hf[:, 2:3], T.hc[:], AxisListType.X, A.add)
-    ph1 = run(PE, [ghi], "mm", T.bh1[:, 0:256], T.gg[:], T.pr[:, 0:256], True, True)
-    ph2 = run(PE, [], "mm", T.bh2[:, 0:256], T.gg[:], T.pr[:, 256:512], True, True)
-    run(PE, [], "mm", T.bt1[:, 0:256], T.lth[:], T.pr[:, 0:256], True, False)
-    run(PE, [], "mm", T.bt2[:, 0:256], T.lth[:], T.pr[:, 256:512], True, False)
-    pt1 = run(PE, [glo], "mm", T.bt1[:, 0:256], T.ltl[:], T.pb[:, 0:256], False, True)
-    pt2 = run(PE, [], "mm", T.bt2[:, 0:256], T.ltl[:], T.pb[:, 256:512], False, True)
-    php = run(PE, [hs], "mm", T.bz[:, 0:1], T.ones[:], T.hf[:, 2:3], True, True)
-    run(SC, [pt1], "act", T.winA[:, 0:256], T.bt1[:, 0:256], COPY)
-    tab = run(SC, [pt2], "act", T.winA[:, 256:512], T.bt2[:, 0:256], COPY)
-    m1 = run(V, [ph1], "ts", T.mask[:, 0:256], T.bh1[:, 0:256], ps, None, A.is_equal)
-    m2 = run(V, [ph2], "ts", T.mask[:, 256:512], T.bh2[:, 0:256], ps, None, A.is_equal)
-    hd = run(V, [php], "ts", T.hd[:, 0:1], T.bz[:, 0:1], float(4096 * 4095 // 2), None, A.add)
-
-    def pend0():
-        a = run(V, [hd], "ts", T.hd[:, 1:2], T.hd[:, 0:1], 7, 7, A.arith_shift_right, A.bitwise_and)
-        run(V, [], "ts", T.hd[:, 2:3], T.hd[:, 0:1], 3, 0x180, A.arith_shift_right, A.bitwise_and)
-        b = run(V, [], "ts", T.hd[:, 3:4], T.hd[:, 0:1], 0x7F, None, A.bitwise_and)
-        c = run(V, [a], "copy", T.hf[:, 1:2], T.hd[:, 1:2])
-        d = run(V, [b], "tt", T.hf[:, 0:1], T.hd[:, 2:3], T.hd[:, 3:4], A.add)
-        run(V, [c], "ts", T.mask[:, 512:528], T.qs[:], T.hf[:, 1:2], None, A.is_equal)
-        return run(V, [d], "ts", T.off[:, 32:33], T.hf[:, 0:1], T.pd[:, 0:1], 256.0, A.add, A.subtract)
-    pending = pend0
     win = [T.winA, T.winB]
     LE = [T.le[:, 128 * q:128 * q + 128] for q in range(16)]
+
+    def table(half, dep, nw):
+        return run(SC, [dep], "act", nw[:, 256 * half:256 * half + 256], (T.bt2 if half else T.bt1)[:, 0:256], COPY)
 
     def gather(w, a, b, deps):
         return run(V, deps, "tt", T.pr[:, 16 * a:16 * b], w.indirect(T.off[:, a:b]), T.mask[:, 16 * a:16 * b], A.mult)
 
-    def extract(a, b, deps):
+    def extract(buf, a, b, deps):
         for q in range(16):
-            e = run(PE, deps, "mm", T.be[:, 0:b - a], LE[q], T.pr[:, 16 * a + q:16 * b:16], q == 0, q == 15)
+            e = run(PE, deps, "mm", buf[:, 0:b - a], LE[q], T.pr[:, 16 * a + q:16 * b:16], q == 0, q == 15)
         return e
 
-    wait(PE, [les])
-    wait(V, [idb])
-    for i in range(10):
-        nF = 1 if i <= 7 else 1 << (i - 7)
-        w, nw = win[i % 2][:], win[(i + 1) % 2]
-        lastr, table = i == 9, not (i == 9 and rank == 0)
-        if table:
-            g1 = gather(w, 0, 16, [tab, offS, m1])
-            pt1 = run(PE, [g1], "mm", T.bt1[:, 0:256], T.lt[:], T.pr[:, 0:256], True, True)
-            run(SC, [pt1], "act", nw[:, 0:256], T.bt1[:, 0:256], COPY)
-            if not lastr:
-                ph1 = run(PE, [], "mm", T.bh1[:, 0:256], T.lh[:], T.pr[:, 0:256], True, True)
-            pF = pending()
-            g2 = gather(w, 16, 32 + nF, [m2, pF])
-            pt2 = run(PE, [g2], "mm", T.bt2[:, 0:256], T.lt[:], T.pr[:, 256:512], True, True)
-            tab = run(SC, [pt2], "act", nw[:, 256:512], T.bt2[:, 0:256], COPY)
-        else:
-            pF = pending()
-            g2 = gather(w, 32, 32 + nF, [tab, pF])
-        new = 32 if i <= 6 else 32 + nF
-        if not lastr:
-            ph2 = run(PE, [], "mm", T.bh2[:, 0:256], T.lh[:], T.pr[:, 256:512], True, True)
-            pe = extract(0, 32 + nF, [])
-            e0 = 32
-        else:
-            pe = extract(32, 32 + nF, [g2])
-            e0 = 0
-        phf = run(PE, [], "mm", T.bhf[:, 0:16 * nF], T.lh[:], T.pr[:, 512:512 + 16 * nF], True, True)
-        if not lastr:
-            m1 = run(V, [ph1, g1], "ts", T.mask[:, 0:256], T.bh1[:, 0:256], ps, None, A.is_equal)
-            m2 = run(V, [ph2, g2], "ts", T.mask[:, 256:512], T.bh2[:, 0:256], ps, None, A.is_equal)
-        if i in hooks:
-            hooks[i]()
-        if not lastr:
-            offS = run(V, [pe], "ts", T.off[:, 0:32], T.be[:, 0:32], 256.0, None, A.add)
+    def tmm(half, dep):
+        return run(PE, [dep], "mm", (T.bt2 if half else T.bt1)[:, 0:256], T.lt[:], T.pr[:, 256 * half:256 * half + 256], True, True)
 
-        def pend(pe=pe, phf=phf, i=i, nF=nF, new=new, e0=e0):
-            sc = T.pd[:, i + 1:i + 2] if i + 1 <= 6 else 256.0
-            run(V, [pe], "ts", T.off[:, new:new + nF], T.be[:, e0:e0 + nF], sc, None, A.add)
-            return run(V, [phf], "ts", T.mask[:, 16 * new:16 * (new + nF)], T.bhf[:, 0:16 * nF], ps, None, A.is_equal)
-        pending = pend
+    def hmm(half, dep, m):
+        return run(PE, [dep], "mm", (T.bh2 if half else T.bh1)[:, 0:256], m, T.pr[:, 256 * half:256 * half + 256], True, True)
+
+    def rows(a, b, dep):
+        return run(PE, [dep], "mm", T.bhf[:, 0:16 * (b - a)], T.lh[:], T.pr[:, 16 * a:16 * b], True, True)
+
+    def maskh(half, *deps):
+        return run(V, deps, "ts", T.mask[:, 256 * half:256 * half + 256], (T.bh2 if half else T.bh1)[:, 0:256], ps, None, A.is_equal)
+
+    def maskf(new, n, *deps):
+        return run(V, deps, "ts", T.mask[:, 16 * new:16 * (new + n)], T.bhf[:, 0:16 * n], ps, None, A.is_equal)
+
+    def offs(a, n, buf, e0, dep, bias=256.0):
+        return run(V, [dep], "ts", T.off[:, a:a + n], buf[:, e0:e0 + n], bias, None, A.add)
+
+    wait(PE, [les, t])
+    wait(V, [idb, t, ("own", 16), ("nxa", 24)])
+    X = T.xi[:]
+    HI, T1, T2, LO, LB = [T.xw[:, 32 * i:32 * i + 32] for i in range(5)]
+    HA, HB, HC = [T.hw[:, 32 * i:32 * i + 32] for i in range(3)]
+    h0 = run(V, [], "ts", HI, X, 7, 7, A.arith_shift_right, A.bitwise_and)
+    run(V, [], "ts", T1, X, 3, 0x180, A.arith_shift_right, A.bitwise_and)
+    t2 = run(V, [], "ts", T2, X, 0x7F, None, A.bitwise_and)
+    ghi = run(V, [h0], "tt", T.pr[:, 0:512], HI.indirect(T.off0[:]), T.diag[:], A.mult)
+    lo = run(V, [t2], "tt", LO, T1, T2, A.add)
+    eq = run(V, [], "tt", HA, X, T.idn[:], A.is_equal)
+    lob = run(V, [lo], "ts", LB, LO, 256.0, None, A.subtract)
+    offS = run(V, [], "copy", T.off[:, 0:32], LO)
+    hb = run(V, [eq], "tt", HB, HA, T.idn[:], A.mult)
+    gla = run(V, [lob], "tt", T.pb[:, 0:256], LB.indirect(T.off0[:, 0:16]), T.diag[:, 0:256], A.mult)
+    glb = run(V, [], "tt", T.pb[:, 256:512], LB.indirect(T.off0[:, 16:32]), T.diag[:, 256:512], A.mult)
+    ph1 = hmm(0, ghi, T.gg[:])
+    ph2 = hmm(1, None, T.gg[:])
+    run(PE, [], "mm", T.bt1[:, 0:256], T.lth[:], T.pr[:, 0:256], True, False)
+    run(PE, [], "mm", T.bt2[:, 0:256], T.lth[:], T.pr[:, 256:512], True, False)
+    pt1 = run(PE, [gla], "mm", T.bt1[:, 0:256], T.ltl[:], T.pb[:, 0:256], False, True)
+    pt2 = run(PE, [glb], "mm", T.bt2[:, 0:256], T.ltl[:], T.pb[:, 256:512], False, True)
+    table(0, pt1, T.winA)
+    tab = table(1, pt2, T.winA)
+    hc = run(V, [hb], "tt", HC, HB, X, A.subtract)
+    m1 = maskh(0, ph1)
+    hs = run(V, [hc], "red", T.hf[:, 2:3], HC, AxisListType.X, A.add)
+    php = run(PE, [hs], "mm", T.bz[:, 0:1], T.ones[:], T.hf[:, 2:3], True, True)
+    m2 = maskh(1, ph2)
+
+    w, nw = win[0][:], win[1]
+    g1 = gather(w, 0, 16, [tab, offS, m1])
+    hd = run(V, [php], "ts", T.hd[:, 0:1], T.bz[:, 0:1], float(4096 * 4095 // 2), None, A.add)
+    g2 = gather(w, 16, 32, [m2])
+    pt1 = tmm(0, g1)
+    ph1 = hmm(0, None, T.lh[:])
+    table(0, pt1, nw)
+    pt2 = tmm(1, g2)
+    tab = table(1, pt2, nw)
+    ph2 = hmm(1, None, T.lh[:])
+    pe = extract(T.be, 0, 32, [])
+    a = run(V, [hd], "ts", T.hd[:, 1:2], T.hd[:, 0:1], 7, 7, A.arith_shift_right, A.bitwise_and)
+    run(V, [], "ts", T.hd[:, 2:3], T.hd[:, 0:1], 3, 0x180, A.arith_shift_right, A.bitwise_and)
+    b = run(V, [], "ts", T.hd[:, 3:4], T.hd[:, 0:1], 0x7F, None, A.bitwise_and)
+    m1 = maskh(0, ph1, g1)
+    c = run(V, [a], "copy", T.hf[:, 1:2], T.hd[:, 1:2])
+    d = run(V, [b], "tt", T.hf[:, 0:1], T.hd[:, 2:3], T.hd[:, 3:4], A.add)
+    m2 = maskh(1, ph2, g2)
+    run(V, [d], "ts", T.off[:, 32:33], T.hf[:, 0:1], col(0), 256.0, A.add, A.subtract)
+    f0 = run(V, [c], "ts", T.mask[:, 512:528], T.qs[:], T.hf[:, 1:2], None, A.is_equal)
+    offS = offs(0, 32, T.be, 0, pe)
+    g3 = gather(w, 32, 33, [f0])
+    phf = rows(32, 33, g3)
+    pef = extract(T.ba, 32, 33, [])
+
+    for i in range(1, 9):
+        nF = 1 if i <= 7 else 2
+        new = 32 if i <= 6 else 32 + nF
+        bias = col(i + 1) if i + 1 <= 6 else 256.0
+        w, nw = win[i % 2][:], win[(i + 1) % 2]
+        g1 = gather(w, 0, 16, [tab, offS, m1])
+        pt1 = tmm(0, g1)
+        ph1 = hmm(0, None, T.lh[:])
+        table(0, pt1, nw)
+        if i == 1:
+            maskf(32, 1, phf)
+            mf = offs(32, 1, T.ba, 0, pef, col(1))
+        g2 = gather(w, 16, 32 + nF, [m2, mf])
+        pt2 = tmm(1, g2)
+        tab = table(1, pt2, nw)
+        ph2 = hmm(1, None, T.lh[:])
+        phf = rows(32, 32 + nF, None)
+        pe = extract(T.be, 0, 32 + nF, [])
+        m1 = maskh(0, ph1, g1)
+        m2 = maskh(1, ph2, g2)
+        maskf(new, nF, phf)
+        offS = offs(0, 32, T.be, 0, pe)
+        mf = offs(new, nF, T.be, 32, pe, bias)
+    w, nw = win[1][:], win[0]
+    g3 = gather(w, 32, 36, [tab, mf])
+    phf = rows(32, 36, g3)
+    pe = extract(T.be, 32, 36, [])
+    if rank:
+        g1 = gather(w, 0, 16, [offS, m1])
+        table(0, tmm(0, g1), nw)
+        g2 = gather(w, 16, 32, [m2])
+        tab = table(1, tmm(1, g2), nw)
+    maskf(36, 4, phf)
+    mf = offs(36, 4, T.be, 0, pe)
     w = win[0][:] if rank else win[1][:, 512:1024]
     steps = max(1, rank)
     for s in range(steps):
-        pF = pending()
-        gF = gather(w, 32, 40, [tab, pF])
+        gF = gather(w, 32, 40, [tab, mf])
         if s < steps - 1:
-            pe = extract(32, 40, [gF])
-            phf = run(PE, [], "mm", T.bhf[:, 0:128], T.lh[:], T.pr[:, 512:640], True, True)
-
-            def pend(pe=pe, phf=phf):
-                run(V, [pe], "ts", T.off[:, 32:40], T.be[:, 0:8], 256.0, None, A.add)
-                return run(V, [phf], "ts", T.mask[:, 512:640], T.bhf[:, 0:128], ps, None, A.is_equal)
-            pending = pend
+            phf = rows(32, 40, gF)
+            pe = extract(T.be, 32, 40, [])
+            maskf(32, 8, phf)
+            mf = offs(32, 8, T.be, 0, pe)
     z = run(PE, [gF], "mm", T.bz[:, 0:128], T.pr[:, 512:640], T.rf[:], True, True)
     zm = run(V, [z], "tt", T.zm[:], T.bz[:, 0:128], T.cm[:], A.mult)
     pl = run(PE, [zm], "mm", T.ba[:, 0:64], T.lq[:], T.zm[:, 0:64], True, True)
-    run(PE, [], "mm", T.bz[:, 128:192], T.lq[:], T.zm[:, 0:64], True, False)
-    pb = run(PE, [], "mm", T.bz[:, 128:192], T.lq128[:], T.zm[:, 64:128], False, True)
-    t = run(V, [pl], "ts", T.li[:, 0:64], T.ba[:, 0:64], 256.0, None, A.add)
-    t = run(V, [t], "ts", T.li[:, 64:128], T.li[:, 0:64], 0x180, None, A.bitwise_and)
-    t = run(V, [t], "ts", T.lf[:, 0:64], T.li[:, 64:128], 7.0, 256.0, A.mult, A.add)
-    t = run(V, [t, pb], "tt", T.lf[:, 64:128], T.lf[:, 0:64], T.bz[:, 128:192], A.add)
-    xo = run(V, [t], "copy", T.xo[:], T.lf[:, 64:128])
+    for b in range(4):
+        pb = run(PE, [], "mm", T.bz[:, 128:192], T.lqs[:, 128 * b:128 * b + 128], T.zm[:, 64 * (b // 2):64 * (b // 2) + 64], b == 0, b == 3)
+    t = run(V, [pl], "ts", T.li[:], T.ba[:, 0:64], 1.0 / 128, (256 - 63.5) / 128, A.mult, A.add)
+    t = run(V, [t, pb], "tt", T.lf[:], T.li[:], T.bz[:, 128:192], A.add)
+    xo = run(V, [t], "ts", T.xo[:], T.lf[:], 896.0, 256.25, A.mult, A.add)
     xs = [("xl0", 16), ("xl1", 16), ("nb", 16), ("rx00", 8), ("rx01", 8), ("rx10", 8), ("rx11", 8), ("fw", 64)]
     wait(SC, xs)
     wait(V, xs)

@@ -3,37 +3,42 @@ from concourse.mybir import AluOpType, AxisListType, ActivationFunctionType
 
 A = AluOpType
 COPY = ActivationFunctionType.Copy
+IDENT = ActivationFunctionType.Identity
 CORES_SIM = 96
-NXE = 2
-W896 = [(0.00111389160156, 0.0000021755695343), (0.142578125, 0.00027942657470703125)]
+NXE = 8
+SP = 18
+N1, N2 = 16 * SP, 512 - 16 * SP
 SCRATCH = {
     "nxs": ("dram", [128, 8], "int32"), "rnx": ("dram", [128, 8], "int32"),
+    "xs": ("sbuf", [128, 1024], "float32"),
     "xall": ("sbuf", [128, 4096], "float32"), "yb": ("sbuf", [128, 1024], "float32"), "rbuf": ("sbuf", [128, 512], "float32"),
     "xi": ("sbuf", [128, 32], "int32"),
     "winA": ("sbuf", [128, 1024], "float32"), "winB": ("sbuf", [128, 1024], "float32"),
     "off": ("sbuf", [128, 40], "uint16"), "off0": ("sbuf", [128, 32], "uint16"), "xo": ("sbuf", [128, 64], "uint16"),
-    "mask": ("sbuf", [128, 640], "bfloat16"), "pr": ("sbuf", [128, 640], "bfloat16"), "pb": ("sbuf", [128, 512], "bfloat16"),
-    "diag": ("sbuf", [128, 512], "bfloat16"),
-    "le": ("sbuf", [128, 2048], "bfloat16"), "gg": ("sbuf", [128, 128], "bfloat16"), "gg0": ("sbuf", [128, 128], "bfloat16"),
+    "mask": ("sbuf", [128, 640], "bfloat16"), "pr": ("sbuf", [128, 640], "bfloat16"),
+    "diag": ("sbuf", [128, 512], "bfloat16"), "m16": ("sbuf", [128, 512], "bfloat16"),
+    "le": ("sbuf", [128, 2048], "bfloat16"), "ltq": ("sbuf", [128, 2048], "bfloat16"),
+    "gg": ("sbuf", [128, 128], "bfloat16"), "gg0": ("sbuf", [128, 128], "bfloat16"),
     "lh": ("sbuf", [128, 128], "bfloat16"), "lt": ("sbuf", [128, 128], "bfloat16"), "ltl": ("sbuf", [128, 128], "bfloat16"),
-    "lth": ("sbuf", [128, 128], "bfloat16"), "lq": ("sbuf", [128, 128], "bfloat16"), "lqs": ("sbuf", [128, 512], "bfloat16"),
+    "lth": ("sbuf", [128, 128], "bfloat16"), "lq": ("sbuf", [128, 128], "bfloat16"), "lq5": ("sbuf", [128, 128], "bfloat16"),
     "rf": ("sbuf", [128, 128], "bfloat16"), "cm": ("sbuf", [128, 128], "bfloat16"), "zm": ("sbuf", [128, 128], "bfloat16"),
     "ones": ("sbuf", [128, 128], "float32"),
     "i_p": ("sbuf", [128, 1], "int32"), "pi": ("sbuf", [128, 16], "int32"), "pf": ("sbuf", [128, 16], "float32"),
-    "pd": ("sbuf", [128, 24], "float32"), "i_m": ("sbuf", [128, 128], "float32"),
-    "i_g": ("sbuf", [128, 128], "float32"), "i_key": ("sbuf", [128, 128], "float32"), "i_low": ("sbuf", [128, 128], "float32"),
-    "i_nk": ("sbuf", [128, 128], "float32"), "i_cm": ("sbuf", [128, 128], "float32"),
+    "pd": ("sbuf", [128, 24], "float32"), "i_m": ("sbuf", [128, 512], "bfloat16"), "dq": ("sbuf", [128, 16], "float32"),
+    "i_g": ("sbuf", [128, 128], "bfloat16"), "i_key": ("sbuf", [128, 128], "bfloat16"), "i_low": ("sbuf", [128, 128], "bfloat16"),
+    "i_nk": ("sbuf", [128, 128], "bfloat16"), "i_cm": ("sbuf", [128, 128], "bfloat16"),
     "i_c": ("sbuf", [128, 32], "float32"), "i_id": ("sbuf", [128, 32], "float32"), "idn": ("sbuf", [128, 32], "float32"),
     "qs": ("sbuf", [128, 16], "float32"),
-    "xw": ("sbuf", [128, 160], "int32"), "hw": ("sbuf", [128, 96], "float32"),
+    "xw": ("sbuf", [128, 128], "int32"), "lof": ("sbuf", [128, 32], "float16"), "hw": ("sbuf", [128, 96], "float32"),
     "hd": ("sbuf", [128, 8], "int32"), "hf": ("sbuf", [128, 8], "float32"),
-    "li": ("sbuf", [128, 64], "int32"), "lf": ("sbuf", [128, 64], "float32"),
     "bh1": ("psum", [128, 512], "float32"), "bh2": ("psum", [128, 512], "float32"), "bt1": ("psum", [128, 512], "float32"),
     "bt2": ("psum", [128, 512], "float32"), "be": ("psum", [128, 512], "float32"), "bhf": ("psum", [128, 512], "float32"),
     "bz": ("psum", [128, 512], "float32"), "ba": ("psum", [128, 512], "float32"),
 }
-SEMAPHORES = ["cv", "cp", "cs", "cg", "nxl", "own", "xl0", "xl1", "nxa", "rnxa", "rq0", "rq1",
+SEMAPHORES = ["cv", "cp", "cs", "cg", "nxl", "own", "xl0", "xl1", "xo", "nxa", "rnxa", "rq0", "rq1", "xp", "pat",
               "rx00", "rx01", "rx10", "rx11", "fw", "nb", "loc", "st"]
+NK = [[1, 2], [0, 8], [2, 8]]
+CM = [[0, 2], [1, 8], [0, 8]]
 
 
 def take(mask, first, n):
@@ -55,18 +60,34 @@ def plan(T, topo):
     return out
 
 
+def piece(r, ch):
+    return 512 * ch + 128 * r
+
+
+def spread(mask, pieces, rid, pid, sem):
+    n = sum((mask >> b) & 1 for b in range(16)) // len(pieces)
+    return [RemoteDMATransfer(dst_ids=[DstId(rid=rid, pnc=pid)], srcs=[i], dsts=[o], dma_engine_mask=take(mask, n * e, n), remote_sem=sem)
+            for e, (o, i) in enumerate(pieces)]
+
+
 def relay_program(g, core, T, topo, r, h, k, dst):
     S = T.sem
     rid, pid, _ = topo.addr(dst)
-    m = topo.mask(core, dst)
-    e8 = take(m, 0, 8)
+    e8 = take(topo.mask(core, dst), 0, 8)
+    buf = T.i_cm if k else T.i_nk
+    g.iota(buf[:], CM if k else NK, 0, 0, allow_small_or_imprecise_dtypes=True).then_inc(S.cg, 1)
+    g.wait_ge(S.cg, 1)
+    g.remote_dma(buf[:], buf[:], S.pat, S.loc, pid, rid, e8)
     g.wait_ge(S.rnxa, NXE)
     g.remote_dma(T.xi[:, 8 * r:8 * r + 8], T.rnx[:], S.nxa, S.loc, pid, rid, e8)
     for q in (0, 1):
         g.wait_ge(S["rq%d" % q], 8)
-        a = 1024 * r + 512 * h + 256 * q
-        g.remote_dma(T.xall[:, a:a + 256], T.rbuf[:, 256 * q:256 * q + 256], S["rx%d%d" % (k, q)], S.loc, pid, rid, e8)
-    g.wait_ge(S.loc, 24)
+        ps = []
+        for c in (2 * q, 2 * q + 1):
+            a = piece(r, 4 * h + c)
+            ps.append((T.xall[:, a:a + 128], T.rbuf[:, 128 * c:128 * c + 128]))
+        g.remote_dma_fused(spread(e8, ps, rid, pid, S["rx%d%d" % (k, q)]), local_sem=S.loc)
+    g.wait_ge(S.loc, 32)
 
 
 def rank_program(g, core, T, topo):
@@ -104,58 +125,72 @@ def rank_program(g, core, T, topo):
     for ch in range(8):
         e = g.sync if ch % 2 == 0 else g.scalar
         e.dma_start(T.nxs[16 * ch:16 * ch + 16, :], T.nx[:, 8 * ch:8 * ch + 8]).then_inc(S.nxl, 16)
-    base = 1024 * rank
-    g.sync.dma_start(T.xall[:, base:base + 512], T.x[:, 0:512]).then_inc(S.xl0, 16)
-    g.scalar.dma_start(T.xall[:, base + 512:base + 1024], T.x[:, 512:1024]).then_inc(S.xl1, 16)
+    g.sync.dma_start(T.xs[:, 0:512], T.x[:, 0:512]).then_inc(S.xl0, 16)
+    g.scalar.dma_start(T.xs[:, 512:1024], T.x[:, 512:1024]).then_inc(S.xl1, 16)
     g.sync.wait_ge(S.nxl, 128)
     g.sync.dma_start(T.xi[:, 8 * rank:8 * rank + 8], T.nxs[:]).then_inc(S.own, 16)
+    g.sync.wait_ge(S.xl0, 16)
+    g.sync.wait_ge(S.xl1, 16)
+    for ch in range(8):
+        a = piece(rank, ch)
+        g.sync.dma_start(T.xall[:, a:a + 128], T.xs[:, 128 * ch:128 * ch + 128]).then_inc(S.xo, 16)
 
-    def iota(buf, pattern, cm=0, flag=True):
+    def iota(buf, pattern, cm=0, base=0, flag=True):
         if flag:
-            return run("g", [], "iota", buf[:], pattern, 0, cm, allow_small_or_imprecise_dtypes=True)
-        return run("g", [], "iota", buf[:], pattern, 0, cm)
-    ip = iota(T.i_p, [[0, 1]], 1, False)
+            return run("g", [], "iota", buf[:], pattern, base, cm, allow_small_or_imprecise_dtypes=True)
+        return run("g", [], "iota", buf[:], pattern, base, cm)
+    nrid, npid, _ = topo.addr(nbr)
+    nm = topo.mask(core, nbr)
+    ip = iota(T.i_p, [[0, 1]], 1, 0, False)
+    if k == 0:
+        iid, ic, buf = iota(T.i_id, [[1024, 4], [16, 8]]), ("xp", 8), T.i_id
+        wait("g", [iid])
+    else:
+        ic, iid, buf = iota(T.i_c, [[1, 32]]), ("xp", 8), T.i_c
+        wait("g", [ic])
+    g.remote_dma(buf[:], buf[:], S.xp, S.loc, npid, nrid, take(nm, 0, 8))
+    loc = 8
     ig = iota(T.i_g, [[1, 8], [0, 16]])
-    ik = iota(T.i_key, [[0, 8], [1, 2], [2, 8]])
-    ic = iota(T.i_c, [[1, 32]])
-    iid = iota(T.i_id, [[1024, 4], [16, 8]])
-    loc = 0
     g.wait_ge(S.nxl, 128)
     ids = [topo.addr(c) for c in me["rel"]]
     g.remote_dma_fused([RemoteDMATransfer(dst_ids=[DstId(rid=i[0], pnc=i[1]) for i in ids], srcs=[T.nxs[:]], dsts=[T.rnx[:], T.rnx[:]],
                                           dma_engine_mask=take(topo.mask(core, me["rel"][0]), 0, NXE), remote_sem=S.rnxa)], local_sem=S.loc)
     loc += NXE
-    nrid, npid, _ = topo.addr(nbr)
-    nm = topo.mask(core, nbr)
     g.remote_dma(T.xi[:, 8 * rank:8 * rank + 8], T.nxs[:], S.nxa, S.loc, npid, nrid, take(nm, 0, 8))
     loc += 8
+    ik = iota(T.i_key, [[0, 8], [1, 2], [2, 8]])
     ilow = iota(T.i_low, [[0, 8], [1, 16]])
-    im = iota(T.i_m, [[1, 128]])
-    ink = iota(T.i_nk, [[1, 2], [0, 8], [2, 8]])
-    icm = iota(T.i_cm, [[0, 2], [1, 8], [0, 8]])
+    im = iota(T.i_m, [[1, 512]], 0, -256)
     g.wait_ge(S.xl0, 16)
     g.wait_ge(S.xl1, 16)
     for q in (0, 1):
         tr = []
         for h in (0, 1):
-            a = base + 512 * h + 256 * q
-            tr.append(RemoteDMATransfer(dst_ids=[DstId(rid=ids[h][0], pnc=ids[h][1])], srcs=[T.xall[:, a:a + 256]],
+            a = 512 * h + 256 * q
+            tr.append(RemoteDMATransfer(dst_ids=[DstId(rid=ids[h][0], pnc=ids[h][1])], srcs=[T.xs[:, a:a + 256]],
                                         dsts=[T.rbuf[:, 256 * q:256 * q + 256]],
                                         dma_engine_mask=take(topo.mask(core, me["rel"][h]), 8 * h, 8), remote_sem=S["rq%d" % q]))
         g.remote_dma_fused(tr, local_sem=S.loc)
         loc += 16
-    g.remote_dma(T.xall[:, base:base + 1024], T.xall[:, base:base + 1024], S.nb, S.loc, npid, nrid, take(nm, 0, 16))
+    n16 = take(nm, 0, 16)
+    ps8 = []
+    for ch in range(8):
+        a = piece(rank, ch)
+        ps8.append((T.xall[:, a:a + 128], T.xs[:, 128 * ch:128 * ch + 128]))
+    g.remote_dma_fused(spread(n16, ps8, nrid, npid, S.nb), local_sem=S.loc)
     loc += 16
     for q in (0, 1):
         for s, fr in enumerate(me["far"]):
             g.wait_ge(S["rx%d%d" % (s, q)], 8)
-            a = 1024 * fr + 512 * k + 256 * q
-            g.remote_dma(T.xall[:, a:a + 256], T.xall[:, a:a + 256], S.fw, S.loc, npid, nrid, take(nm, 0, 16))
+            ps2 = []
+            for c in (2 * q, 2 * q + 1):
+                a = piece(fr, 4 * k + c)
+                ps2.append((T.xall[:, a:a + 128], T.xall[:, a:a + 128]))
+            g.remote_dma_fused(spread(n16, ps2, nrid, npid, S.fw), local_sem=S.loc)
             loc += 16
     g.wait_ge(S.loc, loc)
 
     V, PE, SC = "v", "p", "s"
-    run(V, [], "memset", T.ones[:], 1.0)
     le0 = run(V, [], "memset", T.le[:], 0.0)
     for c, (sh, an) in enumerate([(4, 7), (3, 1), (0, 7), (0, 15), (3, 15)] + [(i, 1) for i in range(7)]):
         t = run(V, [ip], "ts", T.pi[:, c:c + 1], T.i_p[:], sh, an, A.arith_shift_right, A.bitwise_and)
@@ -165,42 +200,42 @@ def rank_program(g, core, T, topo):
     def col(c):
         return T.pd[:, c:c + 1]
     t = run(V, [t], "ts", col(11), pfl, -1.0, 1.0, A.mult, A.add)
-    run(V, [t], "ts", T.pd[:, 0:7], T.pf[:, 5:12], -512.0, 768.0, A.mult, A.add)
+    run(V, [], "memset", T.m16[:], -16.0)
     gg0 = run(V, [t, ig], "ts", T.gg0[:], T.i_g[:], pg, col(11), A.is_equal, A.mult)
     for q in range(16):
         les = run(SC, [gg0, le0], "act", T.le[:, 128 * q + q:128 * q + 128:16], T.gg0[:, q:128:16], COPY)
+    run(V, [], "ts", T.pd[:, 0:7], T.pf[:, 5:12], -512.0, 768.0, A.mult, A.add)
     run(V, [], "ts", col(8), pg, 2.0, None, A.mult)
     run(V, [], "ts", col(9), pg, 2.0, 1.0, A.mult, A.add)
     run(V, [], "ts", col(10), pg, 128.0, pq, A.mult, A.add)
-    t = run(V, [], "ts", col(16), ps, pfl, None, A.mult)
+    sf = run(V, [], "ts", col(16), ps, pfl, None, A.mult)
     run(V, [], "ts", T.gg[:], T.i_g[:], pg, None, A.is_equal)
     run(V, [], "ts", T.lh[:], T.i_g[:], pg, pfl, A.is_equal, A.mult)
-    for b in range(4):
-        u = run(V, [t], "ts", col(12 + b), col(11), 128.0 * b - 256.0, col(16), A.mult, A.add)
-    run(V, [ik], "ts", T.lt[:], T.i_key[:], pk, None, A.is_equal)
-    run(V, [], "ts", T.ltl[:], T.i_key[:], col(8), None, A.is_equal)
+    run(V, [sf, ik], "ts", T.ltl[:], T.i_key[:], col(8), None, A.is_equal)
+    t = run(V, [ilow], "ts", T.dq[:], T.i_low[:, 0:16], pq, None, A.is_equal)
     run(V, [], "ts", T.lth[:], T.i_key[:], col(9), None, A.is_equal)
+    for q in range(16):
+        b = slice(128 * q, 128 * q + 128)
+        if q < 8:
+            run(V, [t], "ts", T.ltq[:, b], T.ltl[:], T.dq[:, q:q + 1], None, A.mult)
+        else:
+            lts = run(SC, [t], "act", T.ltq[:, b], T.ltl[:], COPY, scale=T.dq[:, q:q + 1])
+    run(V, [], "ts", T.lt[:], T.i_key[:], pk, None, A.is_equal)
+    for b in range(4):
+        run(V, [], "ts", T.diag[:, 128 * b:128 * b + 128], T.i_low[:], pq, None, A.is_equal)
     run(V, [ic], "copy", T.off0[:], T.i_c[:])
     run(V, [], "ts", T.qs[:], T.i_c[:, 0:16], 0.0, ps, A.mult, A.add)
     run(V, [iid], "ts", T.idn[:], T.i_id[:], col(10), None, A.add)
-    for b in range(4):
-        run(V, [ilow], "ts", T.diag[:, 128 * b:128 * b + 128], T.i_low[:], pq, None, A.is_equal)
-    for b in range(4):
-        t = run(V, [u, im], "ts", T.winA[:, 512 + 128 * b:640 + 128 * b], T.i_m[:], col(11), col(12 + b), A.mult, A.add)
-    idb = run(SC, [t], "act", T.winB[:, 512:1024], T.winA[:, 512:1024], COPY)
-    run(V, [], "ts", T.lq[:], T.i_low[:], pq, None, A.is_equal)
-    for f in (0, 1):
-        for j in (0, 1):
-            b = 2 * f + j
-            run(V, [], "ts", T.lqs[:, 128 * b:128 * b + 128], T.i_low[:], pq, W896[f][j], A.is_equal, A.mult)
-    run(V, [ink], "ts", T.rf[:], T.i_nk[:], pk, None, A.is_equal)
-    t = run(V, [icm], "ts", T.cm[:], T.i_cm[:], pg, None, A.is_equal)
+    t = run(V, [], "memset", T.ones[:], 1.0)
+    for wb in (T.winA, T.winB):
+        idb = run(SC, [sf, im], "act", wb[:, 512:1024], T.i_m[:], IDENT, bias=col(16), scale=col(11))
 
     win = [T.winA, T.winB]
     LE = [T.le[:, 128 * q:128 * q + 128] for q in range(16)]
+    part = [slice(0, N1), slice(N1, 512)]
 
     def table(half, dep, nw):
-        return run(SC, [dep], "act", nw[:, 256 * half:256 * half + 256], (T.bt2 if half else T.bt1)[:, 0:256], COPY)
+        return run(SC, [dep], "act", nw[:, part[half]], T.bt2[:, 0:N2] if half else T.bt1[:, 0:N1], COPY)
 
     def gather(w, a, b, deps):
         return run(V, deps, "tt", T.pr[:, 16 * a:16 * b], w.indirect(T.off[:, a:b]), T.mask[:, 16 * a:16 * b], A.mult)
@@ -211,74 +246,74 @@ def rank_program(g, core, T, topo):
         return e
 
     def tmm(half, dep):
-        return run(PE, [dep], "mm", (T.bt2 if half else T.bt1)[:, 0:256], T.lt[:], T.pr[:, 256 * half:256 * half + 256], True, True)
+        return run(PE, [dep], "mm", T.bt2[:, 0:N2] if half else T.bt1[:, 0:N1], T.lt[:], T.pr[:, part[half]], True, True)
 
-    def hmm(half, dep, m):
-        return run(PE, [dep], "mm", (T.bh2 if half else T.bh1)[:, 0:256], m, T.pr[:, 256 * half:256 * half + 256], True, True)
+    def hmm(half, dep, m, more=0):
+        n, a = (N2 + 16 * more, N1) if half else (N1, 0)
+        return run(PE, [dep], "mm", (T.bh2 if half else T.bh1)[:, 0:n], m, T.pr[:, a:a + n], True, True)
 
     def rows(a, b, dep):
         return run(PE, [dep], "mm", T.bhf[:, 0:16 * (b - a)], T.lh[:], T.pr[:, 16 * a:16 * b], True, True)
 
-    def maskh(half, *deps):
-        return run(V, deps, "ts", T.mask[:, 256 * half:256 * half + 256], (T.bh2 if half else T.bh1)[:, 0:256], ps, None, A.is_equal)
+    def maskh(half, *deps, more=0):
+        n, a = (N2 + 16 * more, N1) if half else (N1, 0)
+        return run(V, deps, "ts", T.mask[:, a:a + n], (T.bh2 if half else T.bh1)[:, 0:n], ps, None, A.is_equal)
 
-    def maskf(new, n, *deps):
-        return run(V, deps, "ts", T.mask[:, 16 * new:16 * (new + n)], T.bhf[:, 0:16 * n], ps, None, A.is_equal)
+    def maskf(new, n, buf, c0, *deps):
+        return run(V, deps, "ts", T.mask[:, 16 * new:16 * (new + n)], buf[:, c0:c0 + 16 * n], ps, None, A.is_equal)
 
     def offs(a, n, buf, e0, dep, bias=256.0):
         return run(V, [dep], "ts", T.off[:, a:a + n], buf[:, e0:e0 + n], bias, None, A.add)
 
-    wait(PE, [les, t])
-    wait(V, [idb, t, ("own", 16), ("nxa", 24)])
+    wait(PE, [les, lts, t])
+    run(PE, [], "mm", T.bt1[:, 0:512], T.ltl[:], T.m16[:], True, False)
+    wait(V, [t, ("own", 16), ("nxa", 24)])
     X = T.xi[:]
-    HI, T1, T2, LO, LB = [T.xw[:, 32 * i:32 * i + 32] for i in range(5)]
+    HI, T1, T2, LO = [T.xw[:, 32 * i:32 * i + 32] for i in range(4)]
     HA, HB, HC = [T.hw[:, 32 * i:32 * i + 32] for i in range(3)]
-    h0 = run(V, [], "ts", HI, X, 7, 7, A.arith_shift_right, A.bitwise_and)
     run(V, [], "ts", T1, X, 3, 0x180, A.arith_shift_right, A.bitwise_and)
     t2 = run(V, [], "ts", T2, X, 0x7F, None, A.bitwise_and)
+    h0 = run(V, [], "ts", HI, X, 7, 7, A.arith_shift_right, A.bitwise_and)
+    lof = run(V, [t2], "tt", T.lof[:], T1, T2, A.add)
     ghi = run(V, [h0], "tt", T.pr[:, 0:512], HI.indirect(T.off0[:]), T.diag[:], A.mult)
-    lo = run(V, [t2], "tt", LO, T1, T2, A.add)
-    eq = run(V, [], "tt", HA, X, T.idn[:], A.is_equal)
-    lob = run(V, [lo], "ts", LB, LO, 256.0, None, A.subtract)
-    offS = run(V, [], "copy", T.off[:, 0:32], LO)
-    hb = run(V, [eq], "tt", HB, HA, T.idn[:], A.mult)
-    gla = run(V, [lob], "tt", T.pb[:, 0:256], LB.indirect(T.off0[:, 0:16]), T.diag[:, 0:256], A.mult)
-    glb = run(V, [], "tt", T.pb[:, 256:512], LB.indirect(T.off0[:, 16:32]), T.diag[:, 256:512], A.mult)
-    ph1 = hmm(0, ghi, T.gg[:])
+    for q in range(16):
+        run(PE, [lof], "mm", T.bt1[:, q:512:16], T.ltq[:, 128 * q:128 * q + 128], T.lof[:], False, False)
+    pt = run(PE, [ghi], "mm", T.bt1[:, 0:512], T.lth[:], T.pr[:, 0:512], False, True)
+    ph1 = hmm(0, None, T.gg[:])
     ph2 = hmm(1, None, T.gg[:])
-    run(PE, [], "mm", T.bt1[:, 0:256], T.lth[:], T.pr[:, 0:256], True, False)
-    run(PE, [], "mm", T.bt2[:, 0:256], T.lth[:], T.pr[:, 256:512], True, False)
-    pt1 = run(PE, [gla], "mm", T.bt1[:, 0:256], T.ltl[:], T.pb[:, 0:256], False, True)
-    pt2 = run(PE, [glb], "mm", T.bt2[:, 0:256], T.ltl[:], T.pb[:, 256:512], False, True)
-    table(0, pt1, T.winA)
-    tab = table(1, pt2, T.winA)
-    hc = run(V, [hb], "tt", HC, HB, X, A.subtract)
+    run(SC, [pt], "act", T.winA[:, part[0]], T.bt1[:, part[0]], COPY)
+    tab = run(SC, [], "act", T.winA[:, part[1]], T.bt1[:, part[1]], COPY)
+    lo = run(V, [], "tt", LO, T1, T2, A.add)
+    eq = run(V, [], "tt", HA, X, T.idn[:], A.is_equal)
+    offS = run(V, [lo], "copy", T.off[:, 0:32], LO)
     m1 = maskh(0, ph1)
-    hs = run(V, [hc], "red", T.hf[:, 2:3], HC, AxisListType.X, A.add)
-    php = run(PE, [hs], "mm", T.bz[:, 0:1], T.ones[:], T.hf[:, 2:3], True, True)
+    hb = run(V, [eq], "tt", HB, HA, T.idn[:], A.mult)
     m2 = maskh(1, ph2)
+    hc = run(V, [hb], "tt", HC, HB, X, A.subtract)
 
     w, nw = win[0][:], win[1]
-    g1 = gather(w, 0, 16, [tab, offS, m1])
-    hd = run(V, [php], "ts", T.hd[:, 0:1], T.bz[:, 0:1], float(4096 * 4095 // 2), None, A.add)
-    g2 = gather(w, 16, 32, [m2])
+    g1 = gather(w, 0, SP, [idb, tab, offS, m1])
+    hs = run(V, [hc], "red", T.hf[:, 2:3], HC, AxisListType.X, A.add)
+    g2 = gather(w, SP, 32, [m2])
     pt1 = tmm(0, g1)
     ph1 = hmm(0, None, T.lh[:])
     table(0, pt1, nw)
+    php = run(PE, [hs], "mm", T.bz[:, 0:1], T.ones[:], T.hf[:, 2:3], True, True)
     pt2 = tmm(1, g2)
     tab = table(1, pt2, nw)
     ph2 = hmm(1, None, T.lh[:])
     pe = extract(T.be, 0, 32, [])
+    hd = run(V, [php], "ts", T.hd[:, 0:1], T.bz[:, 0:1], float(4096 * 4095 // 2), None, A.add)
+    m1 = maskh(0, ph1, g1)
     a = run(V, [hd], "ts", T.hd[:, 1:2], T.hd[:, 0:1], 7, 7, A.arith_shift_right, A.bitwise_and)
     run(V, [], "ts", T.hd[:, 2:3], T.hd[:, 0:1], 3, 0x180, A.arith_shift_right, A.bitwise_and)
     b = run(V, [], "ts", T.hd[:, 3:4], T.hd[:, 0:1], 0x7F, None, A.bitwise_and)
-    m1 = maskh(0, ph1, g1)
+    m2 = maskh(1, ph2, g2)
     c = run(V, [a], "copy", T.hf[:, 1:2], T.hd[:, 1:2])
     d = run(V, [b], "tt", T.hf[:, 0:1], T.hd[:, 2:3], T.hd[:, 3:4], A.add)
-    m2 = maskh(1, ph2, g2)
+    offS = offs(0, 32, T.be, 0, pe)
     run(V, [d], "ts", T.off[:, 32:33], T.hf[:, 0:1], col(0), 256.0, A.add, A.subtract)
     f0 = run(V, [c], "ts", T.mask[:, 512:528], T.qs[:], T.hf[:, 1:2], None, A.is_equal)
-    offS = offs(0, 32, T.be, 0, pe)
     g3 = gather(w, 32, 33, [f0])
     phf = rows(32, 33, g3)
     pef = extract(T.ba, 32, 33, [])
@@ -288,22 +323,22 @@ def rank_program(g, core, T, topo):
         new = 32 if i <= 6 else 32 + nF
         bias = col(i + 1) if i + 1 <= 6 else 256.0
         w, nw = win[i % 2][:], win[(i + 1) % 2]
-        g1 = gather(w, 0, 16, [tab, offS, m1])
+        g1 = gather(w, 0, SP, [tab, offS, m1])
         pt1 = tmm(0, g1)
         ph1 = hmm(0, None, T.lh[:])
         table(0, pt1, nw)
         if i == 1:
-            maskf(32, 1, phf)
+            maskf(32, 1, T.bhf, 0, phf)
             mf = offs(32, 1, T.ba, 0, pef, col(1))
-        g2 = gather(w, 16, 32 + nF, [m2, mf])
+        g2 = gather(w, SP, 32 + nF, [m2, mf])
         pt2 = tmm(1, g2)
         tab = table(1, pt2, nw)
-        ph2 = hmm(1, None, T.lh[:])
-        phf = rows(32, 32 + nF, None)
+        ph2 = hmm(1, None, T.lh[:], nF)
         pe = extract(T.be, 0, 32 + nF, [])
         m1 = maskh(0, ph1, g1)
-        m2 = maskh(1, ph2, g2)
-        maskf(new, nF, phf)
+        m2 = maskh(1, ph2, g2, more=nF if new == 32 else 0)
+        if new > 32:
+            m2 = maskf(new, nF, T.bh2, N2)
         offS = offs(0, 32, T.be, 0, pe)
         mf = offs(new, nF, T.be, 32, pe, bias)
     w, nw = win[1][:], win[0]
@@ -311,12 +346,15 @@ def rank_program(g, core, T, topo):
     phf = rows(32, 36, g3)
     pe = extract(T.be, 32, 36, [])
     if rank:
-        g1 = gather(w, 0, 16, [offS, m1])
+        g1 = gather(w, 0, SP, [offS, m1])
         table(0, tmm(0, g1), nw)
-        g2 = gather(w, 16, 32, [m2])
+        g2 = gather(w, SP, 32, [m2])
         tab = table(1, tmm(1, g2), nw)
-    maskf(36, 4, phf)
+    maskf(36, 4, T.bhf, 0, phf)
     mf = offs(36, 4, T.be, 0, pe)
+    run(V, [("pat", 16)], "ts", T.rf[:], T.i_nk[:], pk, None, A.is_equal)
+    run(V, [], "ts", T.lq[:], T.i_low[:], pq, None, A.is_equal)
+    late = run(V, [], "ts", T.lq5[:], T.i_low[:], pq, 512.0, A.is_equal, A.mult)
     w = win[0][:] if rank else win[1][:, 512:1024]
     steps = max(1, rank)
     for s in range(steps):
@@ -324,26 +362,24 @@ def rank_program(g, core, T, topo):
         if s < steps - 1:
             phf = rows(32, 40, gF)
             pe = extract(T.be, 32, 40, [])
-            maskf(32, 8, phf)
+            maskf(32, 8, T.bhf, 0, phf)
             mf = offs(32, 8, T.be, 0, pe)
-    z = run(PE, [gF], "mm", T.bz[:, 0:128], T.pr[:, 512:640], T.rf[:], True, True)
-    zm = run(V, [z], "tt", T.zm[:], T.bz[:, 0:128], T.cm[:], A.mult)
-    pl = run(PE, [zm], "mm", T.ba[:, 0:64], T.lq[:], T.zm[:, 0:64], True, True)
-    for b in range(4):
-        pb = run(PE, [], "mm", T.bz[:, 128:192], T.lqs[:, 128 * b:128 * b + 128], T.zm[:, 64 * (b // 2):64 * (b // 2) + 64], b == 0, b == 3)
-    t = run(V, [pl], "ts", T.li[:], T.ba[:, 0:64], 1.0 / 128, (256 - 63.5) / 128, A.mult, A.add)
-    t = run(V, [t, pb], "tt", T.lf[:], T.li[:], T.bz[:, 128:192], A.add)
-    xo = run(V, [t], "ts", T.xo[:], T.lf[:], 896.0, 256.25, A.mult, A.add)
-    xs = [("xl0", 16), ("xl1", 16), ("nb", 16), ("rx00", 8), ("rx01", 8), ("rx10", 8), ("rx11", 8), ("fw", 64)]
+    z = run(PE, [late, gF], "mm", T.bz[:, 0:128], T.pr[:, 512:640], T.rf[:], True, True)
+    cmt = run(V, [], "ts", T.cm[:], T.i_cm[:], pg, None, A.is_equal)
+    zm = run(V, [cmt, z], "tt", T.zm[:], T.bz[:, 0:128], T.cm[:], A.mult)
+    run(PE, [zm], "mm", T.ba[:, 0:64], T.lq[:], T.zm[:, 0:64], True, False)
+    pl = run(PE, [], "mm", T.ba[:, 0:64], T.lq5[:], T.zm[:, 64:128], False, True)
+    xo = run(V, [pl], "ts", T.xo[:], T.ba[:, 0:64], 256.0, None, A.add)
+    xs = [("xo", 128), ("nb", 16), ("rx00", 8), ("rx01", 8), ("rx10", 8), ("rx11", 8), ("fw", 64)]
     wait(SC, xs)
     wait(V, xs)
     got = []
     for q in (0, 1):
         a, b = 256 * q, 512 + 256 * q
-        got.append((a, run(V, [xo], "copy", T.yb[:, a:a + 256], T.xall[:].indirect(T.xo[:, a // 16:a // 16 + 16]))))
-        got.append((b, run(SC, [xo], "act", T.yb[:, b:b + 256], T.xall[:].indirect(T.xo[:, b // 16:b // 16 + 16]), COPY)))
-    for a, tok in got:
-        wait("y", [tok])
-        g.sync.dma_start(T.y[:, a:a + 256], T.yb[:, a:a + 256]).then_inc(S.st, 16)
+        got.append(("y", a, run(V, [xo], "copy", T.yb[:, a:a + 256], T.xall[:].indirect(T.xo[:, a // 16:a // 16 + 16]))))
+        got.append(("s" if q else "y", b, run(SC, [xo], "act", T.yb[:, b:b + 256], T.xall[:].indirect(T.xo[:, b // 16:b // 16 + 16]), COPY)))
+    for e, a, tok in got:
+        wait(e, [tok])
+        eng[e].dma_start(T.y[:, a:a + 256], T.yb[:, a:a + 256]).then_inc(S.st, 16)
     g.sync.wait_ge(S.st, 64)
     wait("v", [("cv", cnt["v"]), ("cp", cnt["p"]), ("cs", cnt["s"]), ("cg", cnt["g"])])

@@ -4,37 +4,27 @@ from concourse.mybir import AluOpType, AxisListType, ActivationFunctionType
 A = AluOpType
 COPY = ActivationFunctionType.Copy
 IDENT = ActivationFunctionType.Identity
+SIGM = ActivationFunctionType.Sigmoid
+STEEP = 160.0
 CORES_SIM = 96
 NXE = 8
-SP = 18
+SP = 20
 N1, N2 = 16 * SP, 512 - 16 * SP
-SCRATCH = {
-    "nxs": ("dram", [128, 8], "int32"), "rnx": ("dram", [128, 8], "int32"),
-    "xs": ("sbuf", [128, 1024], "float32"),
-    "xall": ("sbuf", [128, 4096], "float32"), "yb": ("sbuf", [128, 1024], "float32"), "rbuf": ("sbuf", [128, 512], "float32"),
-    "xi": ("sbuf", [128, 32], "int32"),
-    "winA": ("sbuf", [128, 1024], "float32"), "winB": ("sbuf", [128, 1024], "float32"),
-    "off": ("sbuf", [128, 40], "uint16"), "off0": ("sbuf", [128, 32], "uint16"), "xo": ("sbuf", [128, 64], "uint16"),
-    "mask": ("sbuf", [128, 640], "bfloat16"), "pr": ("sbuf", [128, 640], "bfloat16"),
-    "diag": ("sbuf", [128, 512], "bfloat16"), "m16": ("sbuf", [128, 512], "bfloat16"),
-    "le": ("sbuf", [128, 2048], "bfloat16"), "ltq": ("sbuf", [128, 2048], "bfloat16"),
-    "gg": ("sbuf", [128, 128], "bfloat16"), "gg0": ("sbuf", [128, 128], "bfloat16"),
-    "lh": ("sbuf", [128, 128], "bfloat16"), "lt": ("sbuf", [128, 128], "bfloat16"), "ltl": ("sbuf", [128, 128], "bfloat16"),
-    "lth": ("sbuf", [128, 128], "bfloat16"), "lq": ("sbuf", [128, 128], "bfloat16"), "lq5": ("sbuf", [128, 128], "bfloat16"),
-    "rf": ("sbuf", [128, 128], "bfloat16"), "cm": ("sbuf", [128, 128], "bfloat16"), "zm": ("sbuf", [128, 128], "bfloat16"),
-    "ones": ("sbuf", [128, 128], "float32"),
-    "i_p": ("sbuf", [128, 1], "int32"), "pi": ("sbuf", [128, 16], "int32"), "pf": ("sbuf", [128, 16], "float32"),
-    "pd": ("sbuf", [128, 24], "float32"), "i_m": ("sbuf", [128, 512], "bfloat16"), "dq": ("sbuf", [128, 16], "float32"),
-    "i_g": ("sbuf", [128, 128], "bfloat16"), "i_key": ("sbuf", [128, 128], "bfloat16"), "i_low": ("sbuf", [128, 128], "bfloat16"),
-    "i_nk": ("sbuf", [128, 128], "bfloat16"), "i_cm": ("sbuf", [128, 128], "bfloat16"),
-    "i_c": ("sbuf", [128, 32], "float32"), "i_id": ("sbuf", [128, 32], "float32"), "idn": ("sbuf", [128, 32], "float32"),
-    "qs": ("sbuf", [128, 16], "float32"),
-    "xw": ("sbuf", [128, 128], "int32"), "lof": ("sbuf", [128, 32], "float16"), "hw": ("sbuf", [128, 96], "float32"),
-    "hd": ("sbuf", [128, 8], "int32"), "hf": ("sbuf", [128, 8], "float32"),
-    "bh1": ("psum", [128, 512], "float32"), "bh2": ("psum", [128, 512], "float32"), "bt1": ("psum", [128, 512], "float32"),
-    "bt2": ("psum", [128, 512], "float32"), "be": ("psum", [128, 512], "float32"), "bhf": ("psum", [128, 512], "float32"),
-    "bz": ("psum", [128, 512], "float32"), "ba": ("psum", [128, 512], "float32"),
-}
+SUMHI, SUMLO = 512 * 28, 8 * 256 * 511
+F, B, I = "float32", "bfloat16", "int32"
+SCRATCH = {n: (w, [128, c], d) for n, w, c, d in [
+    ("nxs", "dram", 8, I), ("rnx", "dram", 8, I), ("xs", "sbuf", 1024, F), ("xall", "sbuf", 4096, F), ("yb", "sbuf", 1024, F),
+    ("rbuf", "sbuf", 512, F), ("xi", "sbuf", 32, I), ("winA", "sbuf", 1024, F), ("winB", "sbuf", 1024, F),
+    ("off", "sbuf", 40, "uint16"), ("off0", "sbuf", 32, "uint16"), ("xo", "sbuf", 64, "uint16"), ("mask", "sbuf", 640, B),
+    ("pr", "sbuf", 640, "float16"), ("diag", "sbuf", 512, B), ("lb", "sbuf", 128, B), ("le", "sbuf", 2048, B),
+    ("ltq", "sbuf", 2048, B), ("gg", "sbuf", 128, B), ("lh", "sbuf", 128, B), ("lt", "sbuf", 128, B), ("ltl", "sbuf", 128, B),
+    ("lth", "sbuf", 128, B), ("lq", "sbuf", 128, B), ("lq5", "sbuf", 128, B), ("ka", "sbuf", 384, B), ("kb", "sbuf", 384, B),
+    ("rf", "sbuf", 128, B), ("cm", "sbuf", 128, B), ("zm", "sbuf", 128, B), ("ones", "sbuf", 128, F), ("i_p", "sbuf", 1, I),
+    ("pi", "sbuf", 16, I), ("pf", "sbuf", 16, F), ("pd", "sbuf", 24, F), ("i_m", "sbuf", 512, B), ("dq", "sbuf", 16, F),
+    ("sb", "sbuf", 8, B), ("i_g8", "sbuf", 128, B), ("i_g", "sbuf", 128, B), ("i_key", "sbuf", 128, B), ("i_low", "sbuf", 128, B),
+    ("i_nk", "sbuf", 128, B), ("i_cm", "sbuf", 128, B), ("i_c", "sbuf", 32, F), ("i_id", "sbuf", 32, F), ("idn", "sbuf", 32, F),
+    ("qs", "sbuf", 16, F), ("xw", "sbuf", 128, I), ("lof", "sbuf", 32, "float16"), ("hw", "sbuf", 96, F), ("hx", "sbuf", 64, F),
+    ("hf", "sbuf", 8, F)] + [(n, "psum", 512, F) for n in ("bh1", "bh2", "bt1", "bt2", "be", "bhf", "bz", "ba")]}
 SEMAPHORES = ["cv", "cp", "cs", "cg", "nxl", "own", "xl0", "xl1", "xo", "nxa", "rnxa", "rq0", "rq1", "xp", "pat",
               "rx00", "rx01", "rx10", "rx11", "fw", "nb", "loc", "st"]
 NK = [[1, 2], [0, 8], [2, 8]]
@@ -117,7 +107,7 @@ def rank_program(g, core, T, topo):
         wait(q, deps)
         e = eng[q]
         f = {"memset": lambda: e.memset, "ts": lambda: e.tensor_scalar, "tt": lambda: e.tensor_tensor, "copy": lambda: e.tensor_copy,
-             "red": lambda: e.tensor_reduce, "mm": lambda: e.matmul, "act": lambda: e.activation, "iota": lambda: e.iota}[name]()
+             "mm": lambda: e.matmul, "act": lambda: e.activation, "iota": lambda: e.iota}[name]()
         f(*args, **kw).then_inc(S["c" + q], 1)
         cnt[q] += 1
         return ("c" + q, cnt[q])
@@ -144,23 +134,25 @@ def rank_program(g, core, T, topo):
     ip = iota(T.i_p, [[0, 1]], 1, 0, False)
     if k == 0:
         iid, ic, buf = iota(T.i_id, [[1024, 4], [16, 8]]), ("xp", 8), T.i_id
-        wait("g", [iid])
+        tok = iid
     else:
         ic, iid, buf = iota(T.i_c, [[1, 32]]), ("xp", 8), T.i_c
-        wait("g", [ic])
+        tok = ic
+    ik = iota(T.i_key, [[0, 8], [1, 2], [2, 8]])
+    wait("g", [tok])
     g.remote_dma(buf[:], buf[:], S.xp, S.loc, npid, nrid, take(nm, 0, 8))
     loc = 8
-    ig = iota(T.i_g, [[1, 8], [0, 16]])
     g.wait_ge(S.nxl, 128)
     ids = [topo.addr(c) for c in me["rel"]]
     g.remote_dma_fused([RemoteDMATransfer(dst_ids=[DstId(rid=i[0], pnc=i[1]) for i in ids], srcs=[T.nxs[:]], dsts=[T.rnx[:], T.rnx[:]],
                                           dma_engine_mask=take(topo.mask(core, me["rel"][0]), 0, NXE), remote_sem=S.rnxa)], local_sem=S.loc)
     loc += NXE
+    ilow = iota(T.i_low, [[0, 8], [1, 16]])
     g.remote_dma(T.xi[:, 8 * rank:8 * rank + 8], T.nxs[:], S.nxa, S.loc, npid, nrid, take(nm, 0, 8))
     loc += 8
-    ik = iota(T.i_key, [[0, 8], [1, 2], [2, 8]])
-    ilow = iota(T.i_low, [[0, 8], [1, 16]])
+    ig = iota(T.i_g, [[1, 8], [0, 16]])
     im = iota(T.i_m, [[1, 512]], 0, -256)
+    ig8 = iota(T.i_g8, [[0, 16], [1, 8]])
     g.wait_ge(S.xl0, 16)
     g.wait_ge(S.xl1, 16)
     for q in (0, 1):
@@ -191,48 +183,70 @@ def rank_program(g, core, T, topo):
     g.wait_ge(S.loc, loc)
 
     V, PE, SC = "v", "p", "s"
-    le0 = run(V, [], "memset", T.le[:], 0.0)
-    for c, (sh, an) in enumerate([(4, 7), (3, 1), (0, 7), (0, 15), (3, 15)] + [(i, 1) for i in range(7)]):
+
+    def bit(*which):
+        for i in which:
+            run(V, [ip], "ts", T.pi[:, 5 + i:6 + i], T.i_p[:], i, 1, A.arith_shift_right, A.bitwise_and)
+
+    def bias(i, n):
+        return run(V, [("cv", cnt["v"])], "ts", T.pd[:, i:i + n], T.pi[:, 5 + i:5 + i + n], -512.0, 768.0, A.mult, A.add)
+    for c, (sh, an) in enumerate([(4, 7), (3, 1), (0, 7), (0, 15), (3, 15)]):
         t = run(V, [ip], "ts", T.pi[:, c:c + 1], T.i_p[:], sh, an, A.arith_shift_right, A.bitwise_and)
-    t = run(V, [t], "copy", T.pf[:, 0:12], T.pi[:, 0:12])
+    bit(0)
+    t = run(V, [t], "copy", T.pf[:, 0:5], T.pi[:, 0:5])
+    bit(1, 2)
     pg, pfl, ps, pq, pk = [T.pf[:, c:c + 1] for c in range(5)]
 
     def col(c):
         return T.pd[:, c:c + 1]
-    t = run(V, [t], "ts", col(11), pfl, -1.0, 1.0, A.mult, A.add)
-    run(V, [], "memset", T.m16[:], -16.0)
-    gg0 = run(V, [t, ig], "ts", T.gg0[:], T.i_g[:], pg, col(11), A.is_equal, A.mult)
-    for q in range(16):
-        les = run(SC, [gg0, le0], "act", T.le[:, 128 * q + q:128 * q + 128:16], T.gg0[:, q:128:16], COPY)
-    run(V, [], "ts", T.pd[:, 0:7], T.pf[:, 5:12], -512.0, 768.0, A.mult, A.add)
-    run(V, [], "ts", col(8), pg, 2.0, None, A.mult)
-    run(V, [], "ts", col(9), pg, 2.0, 1.0, A.mult, A.add)
-    run(V, [], "ts", col(10), pg, 128.0, pq, A.mult, A.add)
-    sf = run(V, [], "ts", col(16), ps, pfl, None, A.mult)
-    run(V, [], "ts", T.gg[:], T.i_g[:], pg, None, A.is_equal)
-    run(V, [], "ts", T.lh[:], T.i_g[:], pg, pfl, A.is_equal, A.mult)
-    run(V, [sf, ik], "ts", T.ltl[:], T.i_key[:], col(8), None, A.is_equal)
-    t = run(V, [ilow], "ts", T.dq[:], T.i_low[:, 0:16], pq, None, A.is_equal)
-    run(V, [], "ts", T.lth[:], T.i_key[:], col(9), None, A.is_equal)
+    run(V, [t], "ts", col(16), ps, pfl, None, A.mult)
+    sf = run(V, [], "ts", col(13), ps, -STEEP, STEEP / 2, A.mult, A.add)
+    sgb = run(SC, [sf], "act", T.sb[:, 0:1], col(16), SIGM, bias=-STEEP / 2, scale=STEEP)
+    c8 = run(V, [], "ts", col(8), pg, 2.0, None, A.mult)
+    c11 = run(V, [], "ts", col(11), pfl, -1.0, 1.0, A.mult, A.add)
+    kk = [(col(8), 0.0, T.ltl), (col(8), 1.0, T.lth), (pk, 0.0, T.lt)]
+
+    def keys(b):
+        sc, d, _ = kk[b]
+        run(V, [c8, ik], "ts", T.ka[:, 128 * b:128 * b + 128], T.i_key[:], d, sc, A.subtract, A.is_equal)
+        return run(V, [], "ts", T.kb[:, 128 * b:128 * b + 128], T.i_key[:], d + 2.0, sc, A.subtract, A.is_equal)
+
+    def diff(b, dep):
+        return run(V, [dep], "tt", kk[b][2][:], T.ka[:, 128 * b:128 * b + 128], T.kb[:, 128 * b:128 * b + 128], A.subtract)
+    t = keys(0)
+    keys(1)
+    u = diff(0, t)
+    t = keys(2)
+    diff(1, t)
+    diff(2, None)
+    dq = run(V, [ilow], "ts", T.dq[:], T.i_low[:, 0:16], pq, None, A.is_equal)
+    run(V, [u], "ts", T.lb[:], T.ltl[:], -256.0, None, A.mult)
+    b0 = bias(0, 3)
     for q in range(16):
         b = slice(128 * q, 128 * q + 128)
-        if q < 8:
-            run(V, [t], "ts", T.ltq[:, b], T.ltl[:], T.dq[:, q:q + 1], None, A.mult)
+        if q < 4:
+            run(V, [dq, u], "ts", T.ltq[:, b], T.ltl[:], T.dq[:, q:q + 1], None, A.mult)
         else:
-            lts = run(SC, [t], "act", T.ltq[:, b], T.ltl[:], COPY, scale=T.dq[:, q:q + 1])
-    run(V, [], "ts", T.lt[:], T.i_key[:], pk, None, A.is_equal)
+            lts = run(SC, [dq, u], "act", T.ltq[:, b], T.ltl[:], COPY, scale=T.dq[:, q:q + 1])
     for b in range(4):
         run(V, [], "ts", T.diag[:, 128 * b:128 * b + 128], T.i_low[:], pq, None, A.is_equal)
+        lez = run(SC, [im], "act", T.le[:, 512 * b:512 * b + 512], T.i_m[:], COPY, scale=0.0)
+    run(V, [ig], "ts", T.gg[:], T.i_g[:], pg, None, A.is_equal)
     run(V, [ic], "copy", T.off0[:], T.i_c[:])
+    sc0 = run(V, [], "ts", col(17), ps, 0.0, col(11), A.is_equal, A.mult)
+    c10 = run(V, [], "ts", col(10), pg, 128.0, pq, A.mult, A.add)
+    run(V, [], "ts", T.lh[:], T.i_g[:], pg, pfl, A.is_equal, A.mult)
+    run(V, [b0], "ts", col(19), col(0), float(SUMLO - 256), None, A.add)
+    run(V, [iid, c10], "ts", T.idn[:], T.i_id[:], col(10), None, A.add)
     run(V, [], "ts", T.qs[:], T.i_c[:, 0:16], 0.0, ps, A.mult, A.add)
-    run(V, [iid], "ts", T.idn[:], T.i_id[:], col(10), None, A.add)
     t = run(V, [], "memset", T.ones[:], 1.0)
-    for wb in (T.winA, T.winB):
-        idb = run(SC, [sf, im], "act", wb[:, 512:1024], T.i_m[:], IDENT, bias=col(16), scale=col(11))
 
     win = [T.winA, T.winB]
-    LE = [T.le[:, 128 * q:128 * q + 128] for q in range(16)]
+    LE = [T.le[:, 127 * q:127 * q + 128] for q in range(16)]
     part = [slice(0, N1), slice(N1, 512)]
+
+    def ident(wb):
+        return run(SC, [sgb, sc0, im], "act", wb[:, 512:1024], T.i_m[:], IDENT, bias=T.sb[:, 0:1], scale=col(17))
 
     def table(half, dep, nw):
         return run(SC, [dep], "act", nw[:, part[half]], T.bt2[:, 0:N2] if half else T.bt1[:, 0:N1], COPY)
@@ -255,115 +269,153 @@ def rank_program(g, core, T, topo):
     def rows(a, b, dep):
         return run(PE, [dep], "mm", T.bhf[:, 0:16 * (b - a)], T.lh[:], T.pr[:, 16 * a:16 * b], True, True)
 
-    def maskh(half, *deps, more=0):
-        n, a = (N2 + 16 * more, N1) if half else (N1, 0)
-        return run(V, deps, "ts", T.mask[:, a:a + n], (T.bh2 if half else T.bh1)[:, 0:n], ps, None, A.is_equal)
+    def mask(a, n, buf, c0, *deps):
+        return run(V, deps, "ts", T.mask[:, a:a + n], buf[:, c0:c0 + n], 0.5, ps, A.add, A.is_ge)
 
-    def maskf(new, n, buf, c0, *deps):
-        return run(V, deps, "ts", T.mask[:, 16 * new:16 * (new + n)], buf[:, c0:c0 + 16 * n], ps, None, A.is_equal)
+    def masks(a, n, buf, c0, *deps):
+        return run(SC, deps, "act", T.mask[:, a:a + n], buf[:, c0:c0 + n], SIGM, bias=col(13), scale=STEEP)
 
-    def offs(a, n, buf, e0, dep, bias=256.0):
-        return run(V, [dep], "ts", T.off[:, a:a + n], buf[:, e0:e0 + n], bias, None, A.add)
+    def offs(a, n, buf, e0, dep, by=256.0):
+        return run(V, [dep], "ts", T.off[:, a:a + n], buf[:, e0:e0 + n], by, None, A.add)
 
-    wait(PE, [les, lts, t])
-    run(PE, [], "mm", T.bt1[:, 0:512], T.ltl[:], T.m16[:], True, False)
+    idA = ident(T.winA)
+    wait(PE, [lts, t])
+    run(PE, [], "mm", T.bt1[:, 0:512], T.lb[:], T.diag[:], True, False)
     wait(V, [t, ("own", 16), ("nxa", 24)])
     X = T.xi[:]
     HI, T1, T2, LO = [T.xw[:, 32 * i:32 * i + 32] for i in range(4)]
-    HA, HB, HC = [T.hw[:, 32 * i:32 * i + 32] for i in range(3)]
+    HA = T.hw[:, 0:32]
     run(V, [], "ts", T1, X, 3, 0x180, A.arith_shift_right, A.bitwise_and)
     t2 = run(V, [], "ts", T2, X, 0x7F, None, A.bitwise_and)
     h0 = run(V, [], "ts", HI, X, 7, 7, A.arith_shift_right, A.bitwise_and)
     lof = run(V, [t2], "tt", T.lof[:], T1, T2, A.add)
-    ghi = run(V, [h0], "tt", T.pr[:, 0:512], HI.indirect(T.off0[:]), T.diag[:], A.mult)
+    gh1 = run(V, [h0], "tt", T.pr[:, 0:N1], HI.indirect(T.off0[:, 0:SP]), T.diag[:, 0:N1], A.mult)
+    gh2 = run(V, [], "tt", T.pr[:, N1:512], HI.indirect(T.off0[:, SP:32]), T.diag[:, N1:512], A.mult)
     for q in range(16):
         run(PE, [lof], "mm", T.bt1[:, q:512:16], T.ltq[:, 128 * q:128 * q + 128], T.lof[:], False, False)
-    pt = run(PE, [ghi], "mm", T.bt1[:, 0:512], T.lth[:], T.pr[:, 0:512], False, True)
-    ph1 = hmm(0, None, T.gg[:])
+    ph1 = hmm(0, gh1, T.gg[:])
+    pt = run(PE, [gh2], "mm", T.bt1[:, 0:512], T.lth[:], T.pr[:, 0:512], False, True)
     ph2 = hmm(1, None, T.gg[:])
     run(SC, [pt], "act", T.winA[:, part[0]], T.bt1[:, part[0]], COPY)
     tab = run(SC, [], "act", T.winA[:, part[1]], T.bt1[:, part[1]], COPY)
     lo = run(V, [], "tt", LO, T1, T2, A.add)
-    eq = run(V, [], "tt", HA, X, T.idn[:], A.is_equal)
+    ne = run(V, [], "tt", HA, X, T.idn[:], A.not_equal)
+    m1 = mask(0, N1, T.bh1, 0, ph1)
     offS = run(V, [lo], "copy", T.off[:, 0:32], LO)
-    m1 = maskh(0, ph1)
-    hb = run(V, [eq], "tt", HB, HA, T.idn[:], A.mult)
-    m2 = maskh(1, ph2)
-    hc = run(V, [hb], "tt", HC, HB, X, A.subtract)
+    run(V, [ig8, lez], "ts", T.le[:, 0:2048:16], T.i_g8[:], pg, col(11), A.is_equal, A.mult)
+    run(V, [ne], "tt", T.hw[:, 32:64], HA, HI, A.mult)
+    hc = run(V, [], "tt", T.hw[:, 64:96], HA, LO, A.mult)
+    m2 = mask(N1, N2, T.bh2, 0, ph2)
+    php = run(PE, [hc], "mm", T.bz[:, 0:64], T.ones[:], T.hw[:, 32:96], True, True)
+    run(SC, [php], "act", T.hx[:, 0:32], T.bz[:, 0:32], COPY, accum_out=T.hf[:, 0:1])
+    hs = run(SC, [], "act", T.hx[:, 32:64], T.bz[:, 32:64], COPY, accum_out=T.hf[:, 1:2])
 
-    w, nw = win[0][:], win[1]
-    g1 = gather(w, 0, SP, [idb, tab, offS, m1])
-    hs = run(V, [hc], "red", T.hf[:, 2:3], HC, AxisListType.X, A.add)
+    w, nw = win[0][:, 0:512], win[1]
+    g1 = gather(w, 0, SP, [tab, offS, m1])
     g2 = gather(w, SP, 32, [m2])
     pt1 = tmm(0, g1)
     ph1 = hmm(0, None, T.lh[:])
     table(0, pt1, nw)
-    php = run(PE, [hs], "mm", T.bz[:, 0:1], T.ones[:], T.hf[:, 2:3], True, True)
     pt2 = tmm(1, g2)
     tab = table(1, pt2, nw)
-    ph2 = hmm(1, None, T.lh[:])
     pe = extract(T.be, 0, 32, [])
-    hd = run(V, [php], "ts", T.hd[:, 0:1], T.bz[:, 0:1], float(4096 * 4095 // 2), None, A.add)
-    m1 = maskh(0, ph1, g1)
-    a = run(V, [hd], "ts", T.hd[:, 1:2], T.hd[:, 0:1], 7, 7, A.arith_shift_right, A.bitwise_and)
-    run(V, [], "ts", T.hd[:, 2:3], T.hd[:, 0:1], 3, 0x180, A.arith_shift_right, A.bitwise_and)
-    b = run(V, [], "ts", T.hd[:, 3:4], T.hd[:, 0:1], 0x7F, None, A.bitwise_and)
-    m2 = maskh(1, ph2, g2)
-    c = run(V, [a], "copy", T.hf[:, 1:2], T.hd[:, 1:2])
-    d = run(V, [b], "tt", T.hf[:, 0:1], T.hd[:, 2:3], T.hd[:, 3:4], A.add)
+    ph2 = hmm(1, None, T.lh[:])
+    m2 = masks(N1, N2, T.bh2, 0, ph2, g2)
+    idB = ident(T.winB)
+    f0 = run(V, [idA, hs], "ts", T.mask[:, 512:528], T.qs[:], T.hf[:, 0:1], float(SUMHI), A.add, A.is_le)
+    fo = run(V, [], "ts", T.off[:, 32:33], T.hf[:, 1:2], -1.0, col(19), A.mult, A.add)
+    m1 = mask(0, N1, T.bh1, 0, ph1, g1)
+    g3 = gather(win[0][:], 32, 33, [f0, fo])
     offS = offs(0, 32, T.be, 0, pe)
-    run(V, [d], "ts", T.off[:, 32:33], T.hf[:, 0:1], col(0), 256.0, A.add, A.subtract)
-    f0 = run(V, [c], "ts", T.mask[:, 512:528], T.qs[:], T.hf[:, 1:2], None, A.is_equal)
-    g3 = gather(w, 32, 33, [f0])
     phf = rows(32, 33, g3)
     pef = extract(T.ba, 32, 33, [])
 
     for i in range(1, 9):
         nF = 1 if i <= 7 else 2
         new = 32 if i <= 6 else 32 + nF
-        bias = col(i + 1) if i + 1 <= 6 else 256.0
-        w, nw = win[i % 2][:], win[(i + 1) % 2]
-        g1 = gather(w, 0, SP, [tab, offS, m1])
+        by = col(i + 1) if i + 1 <= 6 else 256.0
+        w, nw = win[i % 2], win[(i + 1) % 2]
+        g1 = gather(w[:, 0:512], 0, SP, [tab, offS, m1])
         pt1 = tmm(0, g1)
         ph1 = hmm(0, None, T.lh[:])
         table(0, pt1, nw)
         if i == 1:
-            maskf(32, 1, T.bhf, 0, phf)
+            mask(512, 16, T.bhf, 0, phf)
             mf = offs(32, 1, T.ba, 0, pef, col(1))
-        g2 = gather(w, SP, 32 + nF, [m2, mf])
+            wait(V, [idB])
+        g2 = gather(w[:], SP, 32 + nF, [m2, mf])
         pt2 = tmm(1, g2)
         tab = table(1, pt2, nw)
-        ph2 = hmm(1, None, T.lh[:], nF)
         pe = extract(T.be, 0, 32 + nF, [])
-        m1 = maskh(0, ph1, g1)
-        m2 = maskh(1, ph2, g2, more=nF if new == 32 else 0)
-        if new > 32:
-            m2 = maskf(new, nF, T.bh2, N2)
+        ph2 = hmm(1, None, T.lh[:], nF)
+        if new == 32:
+            m2 = masks(N1, N2 + 16 * nF, T.bh2, 0, ph2, g2)
+        else:
+            masks(N1, N2, T.bh2, 0, ph2, g2)
+            m2 = masks(16 * new, 16 * nF, T.bh2, N2)
+        if i <= 2:
+            bit(2 * i + 1, 2 * i + 2)
+        m1 = mask(0, N1, T.bh1, 0, ph1, g1)
+        if i <= 2:
+            bias(2 * i + 1, 2)
         offS = offs(0, 32, T.be, 0, pe)
-        mf = offs(new, nF, T.be, 32, pe, bias)
+        mf = offs(new, nF, T.be, 32, pe, by)
+
+    def late_constants():
+        run(V, [("pat", 16)], "ts", T.rf[:], T.i_nk[:], pk, None, A.is_equal)
+        run(V, [], "ts", T.lq[:], T.i_low[:], pq, None, A.is_equal)
+        return run(V, [], "ts", T.lq5[:], T.i_low[:], pq, 512.0, A.is_equal, A.mult)
+
     w, nw = win[1][:], win[0]
-    g3 = gather(w, 32, 36, [tab, mf])
-    phf = rows(32, 36, g3)
-    pe = extract(T.be, 32, 36, [])
-    if rank:
+    if rank < 3:
+        if rank:
+            g1 = gather(w, 0, SP, [tab, offS, m1])
+            table(0, tmm(0, g1), nw)
+        g3 = gather(w, 32, 36, [tab, mf, m2])
+        if rank:
+            g2 = gather(w, SP, 32, [])
+            tab = table(1, tmm(1, g2), nw)
+        phf = rows(32, 36, g3)
+        pe = extract(T.be, 32, 36, [])
+        late = late_constants()
+        mask(576, 64, T.bhf, 0, phf)
+        mf = offs(36, 4, T.be, 0, pe)
+        w = win[0][:] if rank else win[1][:, 512:1024]
+        steps = max(1, rank)
+        for s in range(steps):
+            gF = gather(w, 32, 40, [tab, mf])
+            if s < steps - 1:
+                phf = rows(32, 40, gF)
+                pe = extract(T.be, 32, 40, [])
+                mask(512, 128, T.bhf, 0, phf)
+                mf = offs(32, 8, T.be, 0, pe)
+    else:
+        g1 = gather(w, 0, SP, [tab, offS, m1])
+        pt1 = tmm(0, g1)
+        ph1 = hmm(0, None, T.lh[:])
+        table(0, pt1, nw)
+        g2 = gather(w, SP, 36, [m2, mf])
+        pt2 = tmm(1, g2)
+        tab = table(1, pt2, nw)
+        ph2 = hmm(1, None, T.lh[:], 4)
+        pe = extract(T.be, 0, 36, [])
+        m3 = masks(576, 64, T.bh2, N2, ph2, g2)
+        m2 = masks(N1, N2, T.bh2, 0)
+        m1 = mask(0, N1, T.bh1, 0, ph1, g1)
+        mf = offs(36, 4, T.be, 32, pe)
+        offS = offs(0, 32, T.be, 0, pe)
+        w, nw = win[0][:], win[1]
+        gF = gather(w, 32, 40, [tab, mf, m3])
         g1 = gather(w, 0, SP, [offS, m1])
+        phf = rows(32, 40, gF)
+        pe = extract(T.ba, 32, 40, [])
         table(0, tmm(0, g1), nw)
         g2 = gather(w, SP, 32, [m2])
         tab = table(1, tmm(1, g2), nw)
-    maskf(36, 4, T.bhf, 0, phf)
-    mf = offs(36, 4, T.be, 0, pe)
-    run(V, [("pat", 16)], "ts", T.rf[:], T.i_nk[:], pk, None, A.is_equal)
-    run(V, [], "ts", T.lq[:], T.i_low[:], pq, None, A.is_equal)
-    late = run(V, [], "ts", T.lq5[:], T.i_low[:], pq, 512.0, A.is_equal, A.mult)
-    w = win[0][:] if rank else win[1][:, 512:1024]
-    steps = max(1, rank)
-    for s in range(steps):
-        gF = gather(w, 32, 40, [tab, mf])
-        if s < steps - 1:
-            phf = rows(32, 40, gF)
-            pe = extract(T.be, 32, 40, [])
-            maskf(32, 8, T.bhf, 0, phf)
-            mf = offs(32, 8, T.be, 0, pe)
+        mask(512, 128, T.bhf, 0, phf)
+        mf = offs(32, 8, T.ba, 0, pe)
+        late = late_constants()
+        gF = gather(nw[:], 32, 40, [tab, mf])
     z = run(PE, [late, gF], "mm", T.bz[:, 0:128], T.pr[:, 512:640], T.rf[:], True, True)
     cmt = run(V, [], "ts", T.cm[:], T.i_cm[:], pg, None, A.is_equal)
     zm = run(V, [cmt, z], "tt", T.zm[:], T.bz[:, 0:128], T.cm[:], A.mult)

from concourse.bass import DstId, RemoteDMATransfer
from concourse.mybir import AluOpType, AxisListType, ActivationFunctionType

A = AluOpType
COPY = ActivationFunctionType.Copy
IDENT = ActivationFunctionType.Identity
SIGM = ActivationFunctionType.Sigmoid
STEEP = 160.0
CORES_SIM = 96
NXE = 8
SP = 20
N1, N2 = 16 * SP, 512 - 16 * SP
SUMHI, SUMLO = 512 * 28, 8 * 256 * 511
F, B, I = "float32", "bfloat16", "int32"
SCRATCH = {n: (w, [128, c], d) for n, w, c, d in [
    ("nxs", "dram", 8, I), ("rnx", "dram", 8, I), ("xs", "sbuf", 1024, F), ("xall", "sbuf", 4096, F), ("yb", "sbuf", 1024, F),
    ("rbuf", "sbuf", 512, F), ("xi", "sbuf", 32, I), ("winA", "sbuf", 1024, F), ("winB", "sbuf", 1024, F),
    ("off", "sbuf", 40, "uint16"), ("off0", "sbuf", 32, "uint16"), ("xo", "sbuf", 64, "uint16"), ("mask", "sbuf", 640, B),
    ("pr", "sbuf", 640, "float16"), ("diag", "sbuf", 512, B), ("lb", "sbuf", 128, B), ("le", "sbuf", 2048, B),
    ("ltq", "sbuf", 2048, B), ("gg", "sbuf", 128, B), ("lh", "sbuf", 128, B), ("lt", "sbuf", 128, B), ("ltl", "sbuf", 128, B),
    ("lth", "sbuf", 128, B), ("lq", "sbuf", 128, B), ("lq5", "sbuf", 128, B), ("ka", "sbuf", 384, B), ("kb", "sbuf", 384, B),
    ("rf", "sbuf", 128, B), ("cm", "sbuf", 128, B), ("zm", "sbuf", 128, B), ("ones", "sbuf", 128, F), ("i_p", "sbuf", 1, I),
    ("pi", "sbuf", 16, I), ("pf", "sbuf", 16, F), ("pd", "sbuf", 24, F), ("i_m", "sbuf", 512, B), ("dq", "sbuf", 16, F),
    ("sb", "sbuf", 8, B), ("i_g8", "sbuf", 128, B), ("i_g", "sbuf", 128, B), ("i_key", "sbuf", 128, B), ("i_low", "sbuf", 128, B),
    ("i_nk", "sbuf", 128, B), ("i_cm", "sbuf", 128, B), ("i_c", "sbuf", 32, F), ("i_id", "sbuf", 32, F), ("idn", "sbuf", 32, F),
    ("qs", "sbuf", 16, F), ("xw", "sbuf", 128, I), ("lof", "sbuf", 32, "float16"), ("hw", "sbuf", 96, F), ("hx", "sbuf", 64, F),
    ("hf", "sbuf", 8, F)] + [(n, "psum", 512, F) for n in ("bh1", "bh2", "bt1", "bt2", "be", "bhf", "bz", "ba")]}
SEMAPHORES = ["cv", "cp", "cs", "cg", "nxl", "own", "xl0", "xl1", "xo", "nxa", "rnxa", "rq0", "rq1", "xp", "pat",
              "rx00", "rx01", "rx10", "rx11", "fw", "nb", "loc", "st"]
NK = [[1, 2], [0, 8], [2, 8]]
CM = [[0, 2], [1, 8], [0, 8]]


def take(mask, first, n):
    bits = [b for b in range(16) if (mask >> b) & 1][first:first + n]
    return sum(1 << b for b in bits)


def plan(T, topo):
    cores = list(T.cores)
    out = []
    for r, c in enumerate(cores):
        here = [i for i, d in enumerate(cores) if topo.chip(d) == topo.chip(c)]
        far = [i for i, d in enumerate(cores) if topo.chip(d) != topo.chip(c)]
        k = here.index(r)
        can = [d for d in range(CORES_SIM) if topo.chip(d) == topo.chip(c) and d not in cores
               and all(topo.may_write(d, cores[i]) for i in far)]
        rel = [[d for d in can if topo.die(d) == s][k] for s in (0, 1)]
        out.append({"k": k, "nb": here[1 - k], "far": far, "rel": rel})
    return out


def piece(r, ch):
    return 512 * ch + 128 * r


def spread(mask, pieces, rid, pid, sem):
    n = sum((mask >> b) & 1 for b in range(16)) // len(pieces)
    return [RemoteDMATransfer(dst_ids=[DstId(rid=rid, pnc=pid)], srcs=[i], dsts=[o], dma_engine_mask=take(mask, n * e, n), remote_sem=sem)
            for e, (o, i) in enumerate(pieces)]


def relay_program(g, core, T, topo, r, h, k, dst):
    S = T.sem
    rid, pid, _ = topo.addr(dst)
    e8 = take(topo.mask(core, dst), 0, 8)
    buf = T.i_cm if k else T.i_nk
    g.iota(buf[:], CM if k else NK, 0, 0, allow_small_or_imprecise_dtypes=True).then_inc(S.cg, 1)
    g.wait_ge(S.cg, 1)
    g.remote_dma(buf[:], buf[:], S.pat, S.loc, pid, rid, e8)
    g.wait_ge(S.rnxa, NXE)
    g.remote_dma(T.xi[:, 8 * r:8 * r + 8], T.rnx[:], S.nxa, S.loc, pid, rid, e8)
    for q in (0, 1):
        g.wait_ge(S["rq%d" % q], 8)
        ps = []
        for c in (2 * q, 2 * q + 1):
            a = piece(r, 4 * h + c)
            ps.append((T.xall[:, a:a + 128], T.rbuf[:, 128 * c:128 * c + 128]))
        g.remote_dma_fused(spread(e8, ps, rid, pid, S["rx%d%d" % (k, q)]), local_sem=S.loc)
    g.wait_ge(S.loc, 32)


def rank_program(g, core, T, topo):
    P = plan(T, topo)
    cores = list(T.cores)
    rank = T.rank_of(core)
    S = T.sem
    if rank is None:
        for r, p in enumerate(P):
            for h in (0, 1):
                if p["rel"][h] == core:
                    relay_program(g, core, T, topo, r, h, p["k"], cores[p["far"][h]])
        return
    me = P[rank]
    k, nbr = me["k"], cores[me["nb"]]
    eng = {"v": g.vector, "p": g.tensor, "s": g.scalar, "g": g, "y": g.sync}
    cnt = {"v": 0, "p": 0, "s": 0, "g": 0}
    seen = {}

    def wait(q, deps):
        for d in deps:
            if d is not None and seen.get((q, d[0]), 0) < d[1]:
                eng[q].wait_ge(S[d[0]], d[1])
                seen[(q, d[0])] = d[1]

    def run(q, deps, name, *args, **kw):
        wait(q, deps)
        e = eng[q]
        f = {"memset": lambda: e.memset, "ts": lambda: e.tensor_scalar, "tt": lambda: e.tensor_tensor, "copy": lambda: e.tensor_copy,
             "mm": lambda: e.matmul, "act": lambda: e.activation, "iota": lambda: e.iota}[name]()
        f(*args, **kw).then_inc(S["c" + q], 1)
        cnt[q] += 1
        return ("c" + q, cnt[q])

    for ch in range(8):
        e = g.sync if ch % 2 == 0 else g.scalar
        e.dma_start(T.nxs[16 * ch:16 * ch + 16, :], T.nx[:, 8 * ch:8 * ch + 8]).then_inc(S.nxl, 16)
    g.sync.dma_start(T.xs[:, 0:512], T.x[:, 0:512]).then_inc(S.xl0, 16)
    g.scalar.dma_start(T.xs[:, 512:1024], T.x[:, 512:1024]).then_inc(S.xl1, 16)
    g.sync.wait_ge(S.nxl, 128)
    g.sync.dma_start(T.xi[:, 8 * rank:8 * rank + 8], T.nxs[:]).then_inc(S.own, 16)
    g.sync.wait_ge(S.xl0, 16)
    g.sync.wait_ge(S.xl1, 16)
    for ch in range(8):
        a = piece(rank, ch)
        g.sync.dma_start(T.xall[:, a:a + 128], T.xs[:, 128 * ch:128 * ch + 128]).then_inc(S.xo, 16)

    def iota(buf, pattern, cm=0, base=0, flag=True):
        if flag:
            return run("g", [], "iota", buf[:], pattern, base, cm, allow_small_or_imprecise_dtypes=True)
        return run("g", [], "iota", buf[:], pattern, base, cm)
    nrid, npid, _ = topo.addr(nbr)
    nm = topo.mask(core, nbr)
    ip = iota(T.i_p, [[0, 1]], 1, 0, False)
    if k == 0:
        iid, ic, buf = iota(T.i_id, [[1024, 4], [16, 8]]), ("xp", 8), T.i_id
        tok = iid
    else:
        ic, iid, buf = iota(T.i_c, [[1, 32]]), ("xp", 8), T.i_c
        tok = ic
    ik = iota(T.i_key, [[0, 8], [1, 2], [2, 8]])
    wait("g", [tok])
    g.remote_dma(buf[:], buf[:], S.xp, S.loc, npid, nrid, take(nm, 0, 8))
    loc = 8
    g.wait_ge(S.nxl, 128)
    ids = [topo.addr(c) for c in me["rel"]]
    g.remote_dma_fused([RemoteDMATransfer(dst_ids=[DstId(rid=i[0], pnc=i[1]) for i in ids], srcs=[T.nxs[:]], dsts=[T.rnx[:], T.rnx[:]],
                                          dma_engine_mask=take(topo.mask(core, me["rel"][0]), 0, NXE), remote_sem=S.rnxa)], local_sem=S.loc)
    loc += NXE
    ilow = iota(T.i_low, [[0, 8], [1, 16]])
    g.remote_dma(T.xi[:, 8 * rank:8 * rank + 8], T.nxs[:], S.nxa, S.loc, npid, nrid, take(nm, 0, 8))
    loc += 8
    ig = iota(T.i_g, [[1, 8], [0, 16]])
    im = iota(T.i_m, [[1, 512]], 0, -256)
    ig8 = iota(T.i_g8, [[0, 16], [1, 8]])
    g.wait_ge(S.xl0, 16)
    g.wait_ge(S.xl1, 16)
    for q in (0, 1):
        tr = []
        for h in (0, 1):
            a = 512 * h + 256 * q
            tr.append(RemoteDMATransfer(dst_ids=[DstId(rid=ids[h][0], pnc=ids[h][1])], srcs=[T.xs[:, a:a + 256]],
                                        dsts=[T.rbuf[:, 256 * q:256 * q + 256]],
                                        dma_engine_mask=take(topo.mask(core, me["rel"][h]), 8 * h, 8), remote_sem=S["rq%d" % q]))
        g.remote_dma_fused(tr, local_sem=S.loc)
        loc += 16
    n16 = take(nm, 0, 16)
    ps8 = []
    for ch in range(8):
        a = piece(rank, ch)
        ps8.append((T.xall[:, a:a + 128], T.xs[:, 128 * ch:128 * ch + 128]))
    g.remote_dma_fused(spread(n16, ps8, nrid, npid, S.nb), local_sem=S.loc)
    loc += 16
    for q in (0, 1):
        for s, fr in enumerate(me["far"]):
            g.wait_ge(S["rx%d%d" % (s, q)], 8)
            ps2 = []
            for c in (2 * q, 2 * q + 1):
                a = piece(fr, 4 * k + c)
                ps2.append((T.xall[:, a:a + 128], T.xall[:, a:a + 128]))
            g.remote_dma_fused(spread(n16, ps2, nrid, npid, S.fw), local_sem=S.loc)
            loc += 16
    g.wait_ge(S.loc, loc)

    V, PE, SC = "v", "p", "s"

    def bit(*which):
        for i in which:
            run(V, [ip], "ts", T.pi[:, 5 + i:6 + i], T.i_p[:], i, 1, A.arith_shift_right, A.bitwise_and)

    def bias(i, n):
        return run(V, [("cv", cnt["v"])], "ts", T.pd[:, i:i + n], T.pi[:, 5 + i:5 + i + n], -512.0, 768.0, A.mult, A.add)
    for c, (sh, an) in enumerate([(4, 7), (3, 1), (0, 7), (0, 15), (3, 15)]):
        t = run(V, [ip], "ts", T.pi[:, c:c + 1], T.i_p[:], sh, an, A.arith_shift_right, A.bitwise_and)
    bit(0)
    t = run(V, [t], "copy", T.pf[:, 0:5], T.pi[:, 0:5])
    bit(1, 2)
    pg, pfl, ps, pq, pk = [T.pf[:, c:c + 1] for c in range(5)]

    def col(c):
        return T.pd[:, c:c + 1]
    run(V, [t], "ts", col(16), ps, pfl, None, A.mult)
    sf = run(V, [], "ts", col(13), ps, -STEEP, STEEP / 2, A.mult, A.add)
    sgb = run(SC, [sf], "act", T.sb[:, 0:1], col(16), SIGM, bias=-STEEP / 2, scale=STEEP)
    c8 = run(V, [], "ts", col(8), pg, 2.0, None, A.mult)
    c11 = run(V, [], "ts", col(11), pfl, -1.0, 1.0, A.mult, A.add)
    kk = [(col(8), 0.0, T.ltl), (col(8), 1.0, T.lth), (pk, 0.0, T.lt)]

    def keys(b):
        sc, d, _ = kk[b]
        run(V, [c8, ik], "ts", T.ka[:, 128 * b:128 * b + 128], T.i_key[:], d, sc, A.subtract, A.is_equal)
        return run(V, [], "ts", T.kb[:, 128 * b:128 * b + 128], T.i_key[:], d + 2.0, sc, A.subtract, A.is_equal)

    def diff(b, dep):
        return run(V, [dep], "tt", kk[b][2][:], T.ka[:, 128 * b:128 * b + 128], T.kb[:, 128 * b:128 * b + 128], A.subtract)
    t = keys(0)
    keys(1)
    u = diff(0, t)
    t = keys(2)
    diff(1, t)
    diff(2, None)
    dq = run(V, [ilow], "ts", T.dq[:], T.i_low[:, 0:16], pq, None, A.is_equal)
    run(V, [u], "ts", T.lb[:], T.ltl[:], -256.0, None, A.mult)
    b0 = bias(0, 3)
    for q in range(16):
        b = slice(128 * q, 128 * q + 128)
        if q < 4:
            run(V, [dq, u], "ts", T.ltq[:, b], T.ltl[:], T.dq[:, q:q + 1], None, A.mult)
        else:
            lts = run(SC, [dq, u], "act", T.ltq[:, b], T.ltl[:], COPY, scale=T.dq[:, q:q + 1])
    for b in range(4):
        run(V, [], "ts", T.diag[:, 128 * b:128 * b + 128], T.i_low[:], pq, None, A.is_equal)
        lez = run(SC, [im], "act", T.le[:, 512 * b:512 * b + 512], T.i_m[:], COPY, scale=0.0)
    run(V, [ig], "ts", T.gg[:], T.i_g[:], pg, None, A.is_equal)
    run(V, [ic], "copy", T.off0[:], T.i_c[:])
    sc0 = run(V, [], "ts", col(17), ps, 0.0, col(11), A.is_equal, A.mult)
    c10 = run(V, [], "ts", col(10), pg, 128.0, pq, A.mult, A.add)
    run(V, [], "ts", T.lh[:], T.i_g[:], pg, pfl, A.is_equal, A.mult)
    run(V, [b0], "ts", col(19), col(0), float(SUMLO - 256), None, A.add)
    run(V, [iid, c10], "ts", T.idn[:], T.i_id[:], col(10), None, A.add)
    run(V, [], "ts", T.qs[:], T.i_c[:, 0:16], 0.0, ps, A.mult, A.add)
    t = run(V, [], "memset", T.ones[:], 1.0)

    win = [T.winA, T.winB]
    LE = [T.le[:, 127 * q:127 * q + 128] for q in range(16)]
    part = [slice(0, N1), slice(N1, 512)]

    def ident(wb):
        return run(SC, [sgb, sc0, im], "act", wb[:, 512:1024], T.i_m[:], IDENT, bias=T.sb[:, 0:1], scale=col(17))

    def table(half, dep, nw):
        return run(SC, [dep], "act", nw[:, part[half]], T.bt2[:, 0:N2] if half else T.bt1[:, 0:N1], COPY)

    def gather(w, a, b, deps):
        return run(V, deps, "tt", T.pr[:, 16 * a:16 * b], w.indirect(T.off[:, a:b]), T.mask[:, 16 * a:16 * b], A.mult)

    def extract(buf, a, b, deps):
        for q in range(16):
            e = run(PE, deps, "mm", buf[:, 0:b - a], LE[q], T.pr[:, 16 * a + q:16 * b:16], q == 0, q == 15)
        return e

    def tmm(half, dep):
        return run(PE, [dep], "mm", T.bt2[:, 0:N2] if half else T.bt1[:, 0:N1], T.lt[:], T.pr[:, part[half]], True, True)

    def hmm(half, dep, m, more=0):
        n, a = (N2 + 16 * more, N1) if half else (N1, 0)
        return run(PE, [dep], "mm", (T.bh2 if half else T.bh1)[:, 0:n], m, T.pr[:, a:a + n], True, True)

    def rows(a, b, dep):
        return run(PE, [dep], "mm", T.bhf[:, 0:16 * (b - a)], T.lh[:], T.pr[:, 16 * a:16 * b], True, True)

    def mask(a, n, buf, c0, *deps):
        return run(V, deps, "ts", T.mask[:, a:a + n], buf[:, c0:c0 + n], 0.5, ps, A.add, A.is_ge)

    def masks(a, n, buf, c0, *deps):
        return run(SC, deps, "act", T.mask[:, a:a + n], buf[:, c0:c0 + n], SIGM, bias=col(13), scale=STEEP)

    def offs(a, n, buf, e0, dep, by=256.0):
        return run(V, [dep], "ts", T.off[:, a:a + n], buf[:, e0:e0 + n], by, None, A.add)

    idA = ident(T.winA)
    wait(PE, [lts, t])
    run(PE, [], "mm", T.bt1[:, 0:512], T.lb[:], T.diag[:], True, False)
    wait(V, [t, ("own", 16), ("nxa", 24)])
    X = T.xi[:]
    HI, T1, T2, LO = [T.xw[:, 32 * i:32 * i + 32] for i in range(4)]
    HA = T.hw[:, 0:32]
    run(V, [], "ts", T1, X, 3, 0x180, A.arith_shift_right, A.bitwise_and)
    t2 = run(V, [], "ts", T2, X, 0x7F, None, A.bitwise_and)
    h0 = run(V, [], "ts", HI, X, 7, 7, A.arith_shift_right, A.bitwise_and)
    lof = run(V, [t2], "tt", T.lof[:], T1, T2, A.add)
    gh1 = run(V, [h0], "tt", T.pr[:, 0:N1], HI.indirect(T.off0[:, 0:SP]), T.diag[:, 0:N1], A.mult)
    gh2 = run(V, [], "tt", T.pr[:, N1:512], HI.indirect(T.off0[:, SP:32]), T.diag[:, N1:512], A.mult)
    for q in range(16):
        run(PE, [lof], "mm", T.bt1[:, q:512:16], T.ltq[:, 128 * q:128 * q + 128], T.lof[:], False, False)
    ph1 = hmm(0, gh1, T.gg[:])
    pt = run(PE, [gh2], "mm", T.bt1[:, 0:512], T.lth[:], T.pr[:, 0:512], False, True)
    ph2 = hmm(1, None, T.gg[:])
    run(SC, [pt], "act", T.winA[:, part[0]], T.bt1[:, part[0]], COPY)
    tab = run(SC, [], "act", T.winA[:, part[1]], T.bt1[:, part[1]], COPY)
    lo = run(V, [], "tt", LO, T1, T2, A.add)
    ne = run(V, [], "tt", HA, X, T.idn[:], A.not_equal)
    m1 = mask(0, N1, T.bh1, 0, ph1)
    offS = run(V, [lo], "copy", T.off[:, 0:32], LO)
    run(V, [ig8, lez], "ts", T.le[:, 0:2048:16], T.i_g8[:], pg, col(11), A.is_equal, A.mult)
    run(V, [ne], "tt", T.hw[:, 32:64], HA, HI, A.mult)
    hc = run(V, [], "tt", T.hw[:, 64:96], HA, LO, A.mult)
    m2 = mask(N1, N2, T.bh2, 0, ph2)
    php = run(PE, [hc], "mm", T.bz[:, 0:64], T.ones[:], T.hw[:, 32:96], True, True)
    run(SC, [php], "act", T.hx[:, 0:32], T.bz[:, 0:32], COPY, accum_out=T.hf[:, 0:1])
    hs = run(SC, [], "act", T.hx[:, 32:64], T.bz[:, 32:64], COPY, accum_out=T.hf[:, 1:2])

    w, nw = win[0][:, 0:512], win[1]
    g1 = gather(w, 0, SP, [tab, offS, m1])
    g2 = gather(w, SP, 32, [m2])
    pt1 = tmm(0, g1)
    ph1 = hmm(0, None, T.lh[:])
    table(0, pt1, nw)
    pt2 = tmm(1, g2)
    tab = table(1, pt2, nw)
    pe = extract(T.be, 0, 32, [])
    ph2 = hmm(1, None, T.lh[:])
    m2 = masks(N1, N2, T.bh2, 0, ph2, g2)
    idB = ident(T.winB)
    f0 = run(V, [idA, hs], "ts", T.mask[:, 512:528], T.qs[:], T.hf[:, 0:1], float(SUMHI), A.add, A.is_le)
    fo = run(V, [], "ts", T.off[:, 32:33], T.hf[:, 1:2], -1.0, col(19), A.mult, A.add)
    m1 = mask(0, N1, T.bh1, 0, ph1, g1)
    g3 = gather(win[0][:], 32, 33, [f0, fo])
    offS = offs(0, 32, T.be, 0, pe)
    phf = rows(32, 33, g3)
    pef = extract(T.ba, 32, 33, [])

    for i in range(1, 9):
        nF = 1 if i <= 7 else 2
        new = 32 if i <= 6 else 32 + nF
        by = col(i + 1) if i + 1 <= 6 else 256.0
        w, nw = win[i % 2], win[(i + 1) % 2]
        g1 = gather(w[:, 0:512], 0, SP, [tab, offS, m1])
        pt1 = tmm(0, g1)
        ph1 = hmm(0, None, T.lh[:])
        table(0, pt1, nw)
        if i == 1:
            mask(512, 16, T.bhf, 0, phf)
            mf = offs(32, 1, T.ba, 0, pef, col(1))
            wait(V, [idB])
        g2 = gather(w[:], SP, 32 + nF, [m2, mf])
        pt2 = tmm(1, g2)
        tab = table(1, pt2, nw)
        pe = extract(T.be, 0, 32 + nF, [])
        ph2 = hmm(1, None, T.lh[:], nF)
        if new == 32:
            m2 = masks(N1, N2 + 16 * nF, T.bh2, 0, ph2, g2)
        else:
            masks(N1, N2, T.bh2, 0, ph2, g2)
            m2 = masks(16 * new, 16 * nF, T.bh2, N2)
        if i <= 2:
            bit(2 * i + 1, 2 * i + 2)
        m1 = mask(0, N1, T.bh1, 0, ph1, g1)
        if i <= 2:
            bias(2 * i + 1, 2)
        offS = offs(0, 32, T.be, 0, pe)
        mf = offs(new, nF, T.be, 32, pe, by)

    def late_constants():
        run(V, [("pat", 16)], "ts", T.rf[:], T.i_nk[:], pk, None, A.is_equal)
        run(V, [], "ts", T.lq[:], T.i_low[:], pq, None, A.is_equal)
        return run(V, [], "ts", T.lq5[:], T.i_low[:], pq, 512.0, A.is_equal, A.mult)

    w, nw = win[1][:], win[0]
    if rank < 3:
        if rank:
            g1 = gather(w, 0, SP, [tab, offS, m1])
            table(0, tmm(0, g1), nw)
        g3 = gather(w, 32, 36, [tab, mf, m2])
        if rank:
            g2 = gather(w, SP, 32, [])
            tab = table(1, tmm(1, g2), nw)
        phf = rows(32, 36, g3)
        pe = extract(T.be, 32, 36, [])
        late = late_constants()
        mask(576, 64, T.bhf, 0, phf)
        mf = offs(36, 4, T.be, 0, pe)
        w = win[0][:] if rank else win[1][:, 512:1024]
        steps = max(1, rank)
        for s in range(steps):
            gF = gather(w, 32, 40, [tab, mf])
            if s < steps - 1:
                phf = rows(32, 40, gF)
                pe = extract(T.be, 32, 40, [])
                mask(512, 128, T.bhf, 0, phf)
                mf = offs(32, 8, T.be, 0, pe)
    else:
        g1 = gather(w, 0, SP, [tab, offS, m1])
        pt1 = tmm(0, g1)
        ph1 = hmm(0, None, T.lh[:])
        table(0, pt1, nw)
        g2 = gather(w, SP, 36, [m2, mf])
        pt2 = tmm(1, g2)
        tab = table(1, pt2, nw)
        ph2 = hmm(1, None, T.lh[:], 4)
        pe = extract(T.be, 0, 36, [])
        m3 = masks(576, 64, T.bh2, N2, ph2, g2)
        m2 = masks(N1, N2, T.bh2, 0)
        m1 = mask(0, N1, T.bh1, 0, ph1, g1)
        mf = offs(36, 4, T.be, 32, pe)
        offS = offs(0, 32, T.be, 0, pe)
        w, nw = win[0][:], win[1]
        gF = gather(w, 32, 40, [tab, mf, m3])
        g1 = gather(w, 0, SP, [offS, m1])
        phf = rows(32, 40, gF)
        pe = extract(T.ba, 32, 40, [])
        table(0, tmm(0, g1), nw)
        g2 = gather(w, SP, 32, [m2])
        tab = table(1, tmm(1, g2), nw)
        mask(512, 128, T.bhf, 0, phf)
        mf = offs(32, 8, T.ba, 0, pe)
        late = late_constants()
        gF = gather(nw[:], 32, 40, [tab, mf])
    z = run(PE, [late, gF], "mm", T.bz[:, 0:128], T.pr[:, 512:640], T.rf[:], True, True)
    cmt = run(V, [], "ts", T.cm[:], T.i_cm[:], pg, None, A.is_equal)
    zm = run(V, [cmt, z], "tt", T.zm[:], T.bz[:, 0:128], T.cm[:], A.mult)
    run(PE, [zm], "mm", T.ba[:, 0:64], T.lq[:], T.zm[:, 0:64], True, False)
    pl = run(PE, [], "mm", T.ba[:, 0:64], T.lq5[:], T.zm[:, 64:128], False, True)
    xo = run(V, [pl], "ts", T.xo[:], T.ba[:, 0:64], 256.0, None, A.add)
    xs = [("xo", 128), ("nb", 16), ("rx00", 8), ("rx01", 8), ("rx10", 8), ("rx11", 8), ("fw", 64)]
    wait(SC, xs)
    wait(V, xs)
    got = []
    for q in (0, 1):
        a, b = 256 * q, 512 + 256 * q
        got.append(("y", a, run(V, [xo], "copy", T.yb[:, a:a + 256], T.xall[:].indirect(T.xo[:, a // 16:a // 16 + 16]))))
        got.append(("s" if q else "y", b, run(SC, [xo], "act", T.yb[:, b:b + 256], T.xall[:].indirect(T.xo[:, b // 16:b // 16 + 16]), COPY)))
    for e, a, tok in got:
        wait(e, [tok])
        eng[e].dma_start(T.y[:, a:a + 256], T.yb[:, a:a + 256]).then_inc(S.st, 16)
    g.sync.wait_ge(S.st, 64)
    wait("v", [("cv", cnt["v"]), ("cp", cnt["p"]), ("cs", cnt["s"]), ("cg", cnt["g"])])
